import numpy as np
import ml_dtypes


def mxq(x, axis, fmt="e4m3"):
    dtype, down = {"e4m3": (ml_dtypes.float8_e4m3fn, 7), "e5m2": (ml_dtypes.float8_e5m2, 14)}[fmt]
    v = np.moveaxis(np.asarray(x, np.float32).astype(ml_dtypes.bfloat16).astype(np.float64), axis, -1)
    blocks = v.reshape(v.shape[:-1] + (-1, 32))
    amax = np.abs(blocks).max(-1, keepdims=True)
    byte = np.maximum(np.where(amax > 0, np.frexp(amax)[1] - 1 + 127, 0) - down, 1)
    scale = np.exp2(byte - 127.0)
    codes = (blocks / scale).astype(np.float32).astype(dtype).astype(np.float64)
    return np.moveaxis((codes * scale).reshape(v.shape), -1, axis)


WIDE = False


def mx_kscale(k):
    if not WIDE:
        return np.ones(k)
    levels = np.array([10, -10, 5, -5, 0])
    if k % 512:
        return np.exp2(np.random.permutation(np.resize(levels, k // 32))).repeat(32)
    a = np.empty((k // 512, 16))
    for p in range(k // 512):
        a[p, :8] = np.random.permutation(np.resize(levels, 8))
        for g in range(8):
            far = levels[np.abs(levels - a[p, g]) >= 10]
            a[p, g + 8] = far[np.random.randint(len(far))]
    return np.exp2(a.ravel()).repeat(32)


def f64(x):
    return np.asarray(x).astype(np.float64)


def striped(idx):
    return np.tile(idx.reshape(-1, 16).T, (8, 1)).astype(np.uint16)


def unstriped(offs):
    return offs[:16].T.reshape(-1).astype(np.int64)


E2M1 = np.array([0.0, 0.5, 1.0, 1.5, 2.0, 3.0, 4.0, 6.0, -0.0, -0.5, -1.0, -1.5, -2.0, -3.0, -4.0, -6.0])


def pack_weight(w, fmt):
    k, n = w.shape
    w = f64(np.asarray(w, np.float32).astype(ml_dtypes.bfloat16)).reshape(k // 32, 32, n)
    amax = np.abs(w).max(1)
    if fmt == "e4m3":
        byte = np.frexp(amax)[1] - 1 + 127 - 7
    else:
        mant, ex = np.frexp(amax / 6.0)
        byte = np.where(mant > 0.5, ex, ex - 1) + 127
    byte = np.clip(np.where(amax > 0, byte, 1), 1, 254)
    scaled = (w * np.exp2(127.0 - byte)[:, None, :]).reshape(k, n).astype(np.float32)
    by_word = np.ascontiguousarray(scaled.reshape(k // 512, 128, 4, n).transpose(0, 1, 3, 2))
    if fmt == "e4m3":
        words = by_word.astype(ml_dtypes.float8_e4m3fn).view(np.uint8)
    else:
        c = by_word.astype(ml_dtypes.float4_e2m1fn).view(np.uint8) & 0xF
        words = (c[..., 0::2] | (c[..., 1::2] << 4)).reshape(k // 512, 128, 2 * n)
    return np.ascontiguousarray(words), np.ascontiguousarray(byte.astype(np.uint8).reshape(k // 512, 16, n))


def unpack_weight(words, scales, fmt):
    g, _, n = scales.shape
    words = np.ascontiguousarray(words).reshape(g, 128, n, -1)
    if fmt == "e4m3":
        vals = words.view(ml_dtypes.float8_e4m3fn).astype(np.float64)
    else:
        nib = np.empty((g, 128, n, 4), np.uint8)
        nib[..., 0::2] = words & 0xF
        nib[..., 1::2] = words >> 4
        vals = E2M1[nib]
    vals = vals * np.repeat(np.exp2(scales.astype(np.float64) - 127.0), 8, axis=1)[..., None]
    return vals.transpose(0, 1, 3, 2).reshape(g * 512, n)


def gelu(v):
    return 0.5 * v * (1.0 + np.tanh(np.sqrt(2.0 / np.pi) * (v + 0.044715 * v**3)))


def striped8(idx):
    return np.concatenate([v.reshape(-1, 16).T for v in idx]).astype(np.uint16)


def unstriped8(offs):
    return np.stack([offs[16 * g:16 * g + 16].T.reshape(-1) for g in range(8)]).astype(np.int64)


def runs(v, idx8):
    k = np.arange(v.shape[0])
    return v[k[:, None], idx8[k % 512 // 64]]


K, T, S, H, N = 1024, 2048, 1024, 1024, 384

def setup_inputs():
    n = np.random.standard_normal
    s = mx_kscale(K)[:, None]
    u = mx_kscale(H)[:, None]
    tab_words, tab_scales = pack_weight(n((K, T)) * s, "e4m3")
    wc_words, wc_scales = pack_weight(n((K, H)) / np.sqrt(K) / s, "e2m1")
    wf = (n((K, H)) / np.sqrt(K) / s * u.T).astype(np.float32)
    wl_words, wl_scales = pack_weight(0.5 * n((H, N)) / np.sqrt(H) / u, "e4m3")
    offs = striped8(np.stack([np.random.permutation(T)[:S] for _ in range(8)]))
    obs = (0.7 * n((N, S))).astype(np.float32)
    return {"tab_words": tab_words, "tab_scales": tab_scales, "offs": offs,
            "wc_words": wc_words, "wc_scales": wc_scales, "wf": wf,
            "wl_words": wl_words, "wl_scales": wl_scales, "obs": obs}

def reference(tab_words, tab_scales, offs, wc_words, wc_scales, wf, wl_words, wl_scales, obs):
    v = runs(unpack_weight(tab_words, tab_scales, "e4m3"), unstriped8(offs))
    wc = unpack_weight(wc_words, wc_scales, "e2m1")
    wl = unpack_weight(wl_words, wl_scales, "e4m3")
    a = wc.T @ v
    b = mxq(f64(wf), 0, "e4m3").T @ v
    h = np.sqrt(1.0 + a * a) * b
    level = wl.T @ mxq(h, 0, "e4m3")
    return np.tanh(f64(obs) - level)

@@ -1,0 +1,274 @@
+from contextlib import ExitStack
+
+import concourse.mybir as mybir
+
+K, T, S, H, N = 1024, 2048, 1024, 1024, 384
+FLOPS = 2 * K * H * S * 2 + 2 * H * N * S
+
+F32 = mybir.dt.float32
+BF16 = mybir.dt.bfloat16
+I32 = mybir.dt.int32
+U32 = mybir.dt.uint32
+U16 = mybir.dt.uint16
+U8 = mybir.dt.uint8
+FP8X4 = mybir.dt.float8_e4m3fn_x4
+FP4X4 = mybir.dt.float4_e2m1fn_x4
+ACT = mybir.ActivationFunctionType
+ALU = mybir.AluOpType
+
+P = 128
+PACK = 4
+PASS = P * PACK
+K_PASSES = K // PASS
+R_PASSES = H // PASS
+STEP = 128
+STEPS = S // STEP
+N_TILES = N // P
+QUADS = 4
+GATHERS = [(0, 256), (256, 512), (512, 1024)]
+
+
+def tile_list_surge_gauge_monitor_kernel(
+    tc, tab_words, tab_scales, offs, wc_words, wc_scales, wf, wl_words, wl_scales, obs, out
+):
+    nc = tc.nc
+    with ExitStack() as ctx:
+        keep = ctx.enter_context(tc.tile_pool(name="keep", bufs=1))
+        ring = ctx.enter_context(tc.tile_pool(name="ring", bufs=3))
+        psum_a = ctx.enter_context(tc.psum_pool(name="psum_a", bufs=3))
+        psum_b = ctx.enter_context(tc.psum_pool(name="psum_b", bufs=3))
+        psum_l = ctx.enter_context(tc.psum_pool(name="psum_l", bufs=2))
+
+        lists = keep.tile([P, S // 16], U16, name="lists")
+        nc.sync.dma_start(lists[:], offs)
+
+        warm = keep.tile([P, 8], F32, name="warm")
+        warm_out = keep.tile([P, 8], F32, name="warm_out")
+        late = ctx.enter_context(tc.tile_pool(name="late", bufs=1))
+        late_words = PASS + R_PASSES * N
+        tab_rows = late.tile([P, T], U8, name="tab_rows", offset=4 * late_words - T // 2)
+        wc_rows = keep.tile([P, K_PASSES, H], U8, name="wc_rows")
+        v_scales = [keep.tile([P, S], U8, name="v_scales%d" % a, align_bytes=64) for a in range(K_PASSES)]
+        wl_planes = keep.tile([P, R_PASSES, N], U8, name="wl_planes", align_bytes=64)
+        nc.gpsimd.memset(tab_rows[:].bitcast(I32), 0)
+        nc.vector.memset(wc_rows[:].bitcast(I32), 0)
+        nc.vector.memset(warm[:], 1.0)
+        nc.scalar.activation(warm_out[:], warm[:], ACT.Sqrt, bias=1.0)
+        for a in range(K_PASSES):
+            nc.vector.memset(v_scales[a][:].bitcast(I32), 0)
+        nc.vector.memset(wl_planes[:].bitcast(I32), 0)
+
+        wc_hbm = wc_words.rearrange("a p c -> p a c").bitcast(I32)
+        wc_first = keep.tile([P, PASS], I32, name="wc_first")
+        nc.sync.dma_start(wc_first[:].rearrange("p (a c) -> p a c", a=K_PASSES), wc_hbm[:, :, : PASS // 2])
+        for a in range(K_PASSES):
+            nc.sync.dma_start(tab_rows[a:P:8, :].bitcast(I32), tab_scales[a].bitcast(I32))
+        table = []
+        for a in range(K_PASSES):
+            words = keep.tile([P, T], I32, name="table%d" % a)
+            nc.sync.dma_start(words[:], tab_words[a].rearrange("p t i -> p (t i)").bitcast(I32))
+            table.append(words)
+        for d in range(QUADS):
+            nc.gpsimd.dma_start(
+                wc_rows[32 * d : 32 * d + 4].bitcast(I32),
+                wc_scales[:, 4 * d : 4 * d + 4, :].rearrange("a q c -> q a c").bitcast(I32),
+            )
+        for d in range(QUADS):
+            nc.gpsimd.dma_start(
+                wl_planes[32 * d : 32 * d + 4].bitcast(I32),
+                wl_scales[:, 4 * d : 4 * d + 4, :].rearrange("a q c -> q a c").bitcast(I32),
+            )
+
+        wc_codes = [keep.tile([P, K_PASSES, 2 * PASS], U8, name="wc_codes%d" % b, align_bytes=64) for b in range(R_PASSES)]
+        wc_planes = [keep.tile([P, K_PASSES, PASS], U8, name="wc_planes%d" % b, align_bytes=64) for b in range(R_PASSES)]
+
+        def order_wc_codes(b):
+            nc.vector.tensor_copy(
+                wc_codes[b][:].bitcast(U16).rearrange("p a (t m) -> p a t m", t=PACK),
+                wc_raw[b].bitcast(U16).rearrange("p (a m t) -> p a t m", a=K_PASSES, t=PACK),
+            )
+
+        def order_wc_scales(b):
+            nc.vector.tensor_copy(
+                wc_planes[b][:].rearrange("p a (t m) -> p a t m", t=PACK),
+                wc_rows[:, :, b * PASS : (b + 1) * PASS].rearrange("p a (m t) -> p a t m", t=PACK),
+            )
+
+        wc_raw = {0: wc_first[:]}
+        order_wc_codes(0)
+        picked_rows = keep.tile([P, S], U8, name="picked_rows")
+        nc.vector.tensor_copy(picked_rows[:], tab_rows[:].indirect(lists[:]))
+        for a in range(K_PASSES):
+            for d in range(QUADS):
+                nc.sync.dma_start(
+                    v_scales[a][32 * d : 32 * d + 4, :].bitcast(I32),
+                    picked_rows[32 * d + a : 32 * (d + 1) : 8, :].bitcast(I32),
+                )
+        order_wc_scales(0)
+
+        packed = late.tile([P, late_words], I32, name="packed", offset=0, align_bytes=64)
+        floats = late.tile([P, R_PASSES * K_PASSES * PACK * PASS + N_TILES * S], F32, name="floats", offset=4 * late_words)
+        wf_raw = {}
+
+        def load_wf(b, a):
+            first = (b * K_PASSES + a) * PACK * PASS
+            raw = floats[:, first : first + PACK * PASS].rearrange("p (i c) -> p i c", i=PACK)
+            nc.sync.dma_start(
+                raw, wf[a * PASS : (a + 1) * PASS, b * PASS : (b + 1) * PASS].rearrange("(p i) c -> p i c", i=PACK)
+            )
+            wf_raw[b, a] = raw
+
+        load_wf(0, 0)
+        load_wf(0, 1)
+        wc_raw[1] = packed[:, :PASS]
+        nc.sync.dma_start(wc_raw[1].rearrange("p (a c) -> p a c", a=K_PASSES), wc_hbm[:, :, PASS // 2 :])
+        load_wf(1, 0)
+        load_wf(1, 1)
+        wl_codes = packed[:, PASS:].rearrange("p (b c) -> p b c", b=R_PASSES)
+        nc.sync.dma_start(wl_codes, wl_words.rearrange("a p c i -> p a (c i)").bitcast(I32))
+        observed = floats[:, R_PASSES * K_PASSES * PACK * PASS :].rearrange("p (u j) -> p u j", u=N_TILES)
+        nc.sync.dma_start(observed, obs.rearrange("(u p) j -> p u j", p=P))
+
+        v_codes = [keep.tile([P, S], U32, name="v_codes%d" % a, align_bytes=64) for a in range(K_PASSES)]
+
+        def gather(lo, hi):
+            for a in range(K_PASSES):
+                nc.vector.tensor_copy(
+                    v_codes[a][:, lo:hi], table[a][:].bitcast(U32).indirect(lists[:, lo // 16 : hi // 16])
+                )
+
+        squares = {}
+        speeds = {}
+
+        def current(b, s):
+            cols = slice(s * STEP, (s + 1) * STEP)
+            bank = psum_a.tile([P, PACK, STEP], F32, name="a_bank")
+            for t in range(PACK):
+                for a in range(K_PASSES):
+                    nc.tensor.matmul_mx(
+                        out=bank[:, t, :],
+                        lhsT=wc_codes[b][:, a, 2 * P * t : 2 * P * (t + 1)].bitcast(FP4X4),
+                        lhsT_scale=wc_planes[b][:, a, P * t : P * (t + 1)],
+                        rhs=v_codes[a][:, cols].bitcast(FP8X4),
+                        rhs_scale=v_scales[a][:, cols],
+                        start=(a == 0),
+                        stop=(a == K_PASSES - 1),
+                    )
+            square = keep.tile([P, STEP, PACK], F32, name="square%d_%d" % (b, s))
+            nc.scalar.activation(square[:], bank[:].rearrange("p t j -> p j t"), ACT.Square)
+            squares[b, s] = square
+
+        def speed(b, s):
+            root = keep.tile([P, STEP, PACK], F32, name="speed%d_%d" % (b, s))
+            nc.scalar.activation(root[:], squares[b, s][:], ACT.Sqrt, bias=1.0)
+            speeds[b, s] = root
+
+        wf_codes = {}
+        wf_planes = {}
+        wf_round = {}
+
+        def round_wf(b, a, copy):
+            rounded = keep.tile([P, PACK, P, PACK], BF16, name="wf_round%d%d" % (b, a), align_bytes=64)
+            copy(
+                rounded[:].rearrange("p t m i -> p m i t"),
+                wf_raw[b, a].rearrange("p i (m t) -> p m i t", t=PACK),
+            )
+            wf_round[b, a] = rounded
+
+        def quantise_wf(b, a):
+            codes = keep.tile([P, PASS], U32, name="wf_codes%d%d" % (b, a), align_bytes=64)
+            plane = keep.tile([P, PASS], U8, name="wf_plane%d%d" % (b, a), align_bytes=64)
+            nc.vector.quantize_mx(
+                out=codes[:].bitcast(FP8X4),
+                scales=plane[:],
+                in_=wf_round[b, a][:].rearrange("p t m i -> p (t m i)"),
+            )
+            wf_codes[b, a] = codes
+            wf_planes[b, a] = plane
+
+        drags = {}
+        h_codes = {}
+        h_planes = {}
+
+        def drag(b, s):
+            cols = slice(s * STEP, (s + 1) * STEP)
+            bank = psum_b.tile([P, PACK, STEP], F32, name="b_bank")
+            for t in range(PACK):
+                for a in range(K_PASSES):
+                    nc.tensor.matmul_mx(
+                        out=bank[:, t, :],
+                        lhsT=wf_codes[b, a][:, P * t : P * (t + 1)].bitcast(FP8X4),
+                        lhsT_scale=wf_planes[b, a][:, P * t : P * (t + 1)],
+                        rhs=v_codes[a][:, cols].bitcast(FP8X4),
+                        rhs_scale=v_scales[a][:, cols],
+                        start=(a == 0),
+                        stop=(a == K_PASSES - 1),
+                    )
+            h = keep.tile([P, STEP, PACK], BF16, name="drag%d_%d" % (b, s), align_bytes=64)
+            nc.vector.tensor_tensor(h[:], bank[:].rearrange("p t j -> p j t"), speeds[b, s][:], ALU.mult)
+            drags[b, s] = h
+
+        def quantise_drag(b, s):
+            codes = keep.tile([P, STEP], U32, name="h_codes%d_%d" % (b, s), align_bytes=64)
+            plane = keep.tile([P, STEP], U8, name="h_plane%d_%d" % (b, s), align_bytes=64)
+            nc.vector.quantize_mx(
+                out=codes[:].bitcast(FP8X4), scales=plane[:], in_=drags[b, s][:].rearrange("p j t -> p (j t)")
+            )
+            h_codes[b, s] = codes
+            h_planes[b, s] = plane
+
+        def innovation(s):
+            cols = slice(s * STEP, (s + 1) * STEP)
+            bank = psum_l.tile([P, N_TILES, STEP], F32, name="level_bank")
+            for u in range(N_TILES):
+                for b in range(R_PASSES):
+                    nc.tensor.matmul_mx(
+                        out=bank[:, u, :],
+                        lhsT=wl_codes[:, b, P * u : P * (u + 1)].bitcast(FP8X4),
+                        lhsT_scale=wl_planes[:, b, P * u : P * (u + 1)],
+                        rhs=h_codes[b, s][:].bitcast(FP8X4),
+                        rhs_scale=h_planes[b, s][:],
+                        start=(b == 0),
+                        stop=(b == R_PASSES - 1),
+                    )
+            gap = ring.tile([P, N_TILES, STEP], F32, name="gap")
+            nc.vector.tensor_tensor(gap[:], observed[:, :, cols], bank[:], ALU.subtract)
+            bounded = ring.tile([P, N_TILES, STEP], F32, name="bounded")
+            nc.scalar.activation(bounded[:], gap[:], ACT.Tanh)
+            nc.sync.dma_start(out.rearrange("(u p) j -> p u j", p=P)[:, :, cols], bounded[:])
+
+        gather(*GATHERS[0])
+        gather(*GATHERS[1])
+        gather(*GATHERS[2])
+        order_wc_scales(1)
+        units = [(b, s) for b in range(R_PASSES) for s in range(STEPS)]
+        lag = 4
+        for n in range(STEPS):
+            current(*units[n])
+            if n >= lag:
+                speed(*units[n - lag])
+        round_wf(0, 0, nc.vector.tensor_copy)
+        round_wf(0, 1, nc.vector.tensor_copy)
+        quantise_wf(0, 0)
+        order_wc_codes(1)
+        quantise_wf(0, 1)
+        round_wf(1, 0, nc.vector.tensor_copy)
+        round_wf(1, 1, nc.scalar.copy)
+        quantise_wf(1, 0)
+        for s in range(STEPS):
+            current(1, s)
+            speed(*units[STEPS + s - lag])
+            drag(0, s)
+            if s > 0:
+                quantise_drag(0, s - 1)
+        quantise_wf(1, 1)
+        quantise_drag(0, STEPS - 1)
+        for s in range(STEPS + 2):
+            if s < lag:
+                speed(1, STEPS - lag + s)
+            if s < STEPS:
+                drag(1, s)
+            if 0 < s <= STEPS:
+                quantise_drag(1, s - 1)
+            if s > 1:
+                innovation(s - 2)

@@ -34,7 +34,7 @@ def tile_list_surge_gauge_monitor_kernel(
     nc = tc.nc
     with ExitStack() as ctx:
         keep = ctx.enter_context(tc.tile_pool(name="keep", bufs=1))
-        ring = ctx.enter_context(tc.tile_pool(name="ring", bufs=3))
+        ring = ctx.enter_context(tc.tile_pool(name="ring", bufs=5))
         psum_a = ctx.enter_context(tc.psum_pool(name="psum_a", bufs=3))
         psum_b = ctx.enter_context(tc.psum_pool(name="psum_b", bufs=3))
         psum_l = ctx.enter_context(tc.psum_pool(name="psum_l", bufs=2))
@@ -45,68 +45,74 @@ def tile_list_surge_gauge_monitor_kernel(
         warm = keep.tile([P, 8], F32, name="warm")
         warm_out = keep.tile([P, 8], F32, name="warm_out")
         late = ctx.enter_context(tc.tile_pool(name="late", bufs=1))
-        late_words = PASS + R_PASSES * N
+        late_words = R_PASSES * N + R_PASSES * N // 4
         tab_rows = late.tile([P, T], U8, name="tab_rows", offset=4 * late_words - T // 2)
         wc_rows = keep.tile([P, K_PASSES, H], U8, name="wc_rows")
         v_scales = [keep.tile([P, S], U8, name="v_scales%d" % a, align_bytes=64) for a in range(K_PASSES)]
-        wl_planes = keep.tile([P, R_PASSES, N], U8, name="wl_planes", align_bytes=64)
         nc.gpsimd.memset(tab_rows[:].bitcast(I32), 0)
         nc.vector.memset(wc_rows[:].bitcast(I32), 0)
         nc.vector.memset(warm[:], 1.0)
         nc.scalar.activation(warm_out[:], warm[:], ACT.Sqrt, bias=1.0)
-        for a in range(K_PASSES):
-            nc.vector.memset(v_scales[a][:].bitcast(I32), 0)
-        nc.vector.memset(wl_planes[:].bitcast(I32), 0)
+        nc.vector.memset(v_scales[1][:].bitcast(I32), 0)
 
         wc_hbm = wc_words.rearrange("a p c -> p a c").bitcast(I32)
-        wc_first = keep.tile([P, PASS], I32, name="wc_first")
-        nc.sync.dma_start(wc_first[:].rearrange("p (a c) -> p a c", a=K_PASSES), wc_hbm[:, :, : PASS // 2])
-        for a in range(K_PASSES):
-            nc.sync.dma_start(tab_rows[a:P:8, :].bitcast(I32), tab_scales[a].bitcast(I32))
-        table = []
-        for a in range(K_PASSES):
-            words = keep.tile([P, T], I32, name="table%d" % a)
-            nc.sync.dma_start(words[:], tab_words[a].rearrange("p t i -> p (t i)").bitcast(I32))
-            table.append(words)
-        for d in range(QUADS):
-            nc.gpsimd.dma_start(
-                wc_rows[32 * d : 32 * d + 4].bitcast(I32),
-                wc_scales[:, 4 * d : 4 * d + 4, :].rearrange("a q c -> q a c").bitcast(I32),
-            )
-        for d in range(QUADS):
-            nc.gpsimd.dma_start(
-                wl_planes[32 * d : 32 * d + 4].bitcast(I32),
-                wl_scales[:, 4 * d : 4 * d + 4, :].rearrange("a q c -> q a c").bitcast(I32),
+        wc_raw = [keep.tile([P, PASS], I32, name="wc_raw%d" % b) for b in range(R_PASSES)]
+        table = [keep.tile([P, T], I32, name="table%d" % a) for a in range(K_PASSES)]
+
+        def load_wc(b):
+            nc.sync.dma_start(
+                wc_raw[b][:].rearrange("p (a c) -> p a c", a=K_PASSES),
+                wc_hbm[:, :, b * PASS // 2 : (b + 1) * PASS // 2],
             )
 
-        wc_codes = [keep.tile([P, K_PASSES, 2 * PASS], U8, name="wc_codes%d" % b, align_bytes=64) for b in range(R_PASSES)]
-        wc_planes = [keep.tile([P, K_PASSES, PASS], U8, name="wc_planes%d" % b, align_bytes=64) for b in range(R_PASSES)]
+        def load_table(a):
+            nc.sync.dma_start(table[a][:], tab_words[a].rearrange("p t i -> p (t i)").bitcast(I32))
+
+        def load_planes(planes, rows):
+            for d in range(QUADS):
+                nc.sync.dma_start(
+                    planes[32 * d : 32 * d + 4].bitcast(I32),
+                    rows[:, 4 * d : 4 * d + 4, :].rearrange("a q c -> q a c").bitcast(I32),
+                )
+
+        load_wc(0)
+        for e in range(2):
+            nc.sync.dma_start(tab_rows[e:P:16, :].bitcast(I32), tab_scales[0, e::2, :].bitcast(I32))
+        nc.sync.dma_start(tab_rows[2:P:8, :].bitcast(I32), tab_scales[1].bitcast(I32))
+        load_table(0)
+        load_planes(wc_rows, wc_scales)
+        load_wc(1)
+        load_table(1)
+
+        wc_codes = {0: keep.tile([P, K_PASSES, 2 * PASS], U8, name="wc_codes0", align_bytes=64)[:]}
+        mid = ctx.enter_context(tc.tile_pool(name="mid", bufs=1))
+        wc_planes = {0: keep.tile([P, K_PASSES, PASS], U8, name="wc_planes0", align_bytes=64)[:]}
 
         def order_wc_codes(b):
             nc.vector.tensor_copy(
-                wc_codes[b][:].bitcast(U16).rearrange("p a (t m) -> p a t m", t=PACK),
-                wc_raw[b].bitcast(U16).rearrange("p (a m t) -> p a t m", a=K_PASSES, t=PACK),
+                wc_codes[b].bitcast(U16).rearrange("p a (t m) -> p a t m", t=PACK),
+                wc_raw[b][:].bitcast(U16).rearrange("p (a m t) -> p a t m", a=K_PASSES, t=PACK),
             )
 
         def order_wc_scales(b):
             nc.vector.tensor_copy(
-                wc_planes[b][:].rearrange("p a (t m) -> p a t m", t=PACK),
+                wc_planes[b].rearrange("p a (t m) -> p a t m", t=PACK),
                 wc_rows[:, :, b * PASS : (b + 1) * PASS].rearrange("p a (m t) -> p a t m", t=PACK),
             )
 
-        wc_raw = {0: wc_first[:]}
         order_wc_codes(0)
-        picked_rows = keep.tile([P, S], U8, name="picked_rows")
+        held_words = 1280
+        picked_rows = mid.tile([P, S], U8, name="picked_rows", offset=4 * held_words - S // 2, align_bytes=64)
         nc.vector.tensor_copy(picked_rows[:], tab_rows[:].indirect(lists[:]))
-        for a in range(K_PASSES):
-            for d in range(QUADS):
-                nc.sync.dma_start(
-                    v_scales[a][32 * d : 32 * d + 4, :].bitcast(I32),
-                    picked_rows[32 * d + a : 32 * (d + 1) : 8, :].bitcast(I32),
-                )
-        order_wc_scales(0)
+        picked = picked_rows[:].bitcast(I32)
+        nc.vector.tensor_copy(v_scales[0][:].bitcast(I32), picked)
+        for r in range(4):
+            nc.sync.dma_start(v_scales[1][r:P:32, :].bitcast(I32), picked[8 * r + 2 : P : 32, :])
+        for e in range(2):
+            nc.sync.dma_start(v_scales[0][2 + e : P : 32, :].bitcast(I32), picked[16 + e : P : 32, :])
 
         packed = late.tile([P, late_words], I32, name="packed", offset=0, align_bytes=64)
+        order_wc_scales(0)
         floats = late.tile([P, R_PASSES * K_PASSES * PACK * PASS + N_TILES * S], F32, name="floats", offset=4 * late_words)
         wf_raw = {}
 
@@ -120,22 +126,28 @@ def tile_list_surge_gauge_monitor_kernel(
 
         load_wf(0, 0)
         load_wf(0, 1)
-        wc_raw[1] = packed[:, :PASS]
-        nc.sync.dma_start(wc_raw[1].rearrange("p (a c) -> p a c", a=K_PASSES), wc_hbm[:, :, PASS // 2 :])
         load_wf(1, 0)
         load_wf(1, 1)
-        wl_codes = packed[:, PASS:].rearrange("p (b c) -> p b c", b=R_PASSES)
+        wl_codes = packed[:, : R_PASSES * N].rearrange("p (b c) -> p b c", b=R_PASSES)
         nc.sync.dma_start(wl_codes, wl_words.rearrange("a p c i -> p a (c i)").bitcast(I32))
+        nc.gpsimd.memset(packed[:, R_PASSES * N :], 0)
+        wl_planes = packed[:, R_PASSES * N :].bitcast(U8).rearrange("p (b c) -> p b c", b=R_PASSES)
+        load_planes(wl_planes, wl_scales)
         observed = floats[:, R_PASSES * K_PASSES * PACK * PASS :].rearrange("p (u j) -> p u j", u=N_TILES)
         nc.sync.dma_start(observed, obs.rearrange("(u p) j -> p u j", p=P))
 
-        v_codes = [keep.tile([P, S], U32, name="v_codes%d" % a, align_bytes=64) for a in range(K_PASSES)]
+        wc_second = mid.tile([P, 3 * K_PASSES * PASS], U8, name="wc_second", align_bytes=64, offset=4 * held_words)
+        wc_codes[1] = wc_second[:, : 2 * K_PASSES * PASS].rearrange("p (a c) -> p a c", a=K_PASSES)
+        wc_planes[1] = wc_second[:, 2 * K_PASSES * PASS :].rearrange("p (a c) -> p a c", a=K_PASSES)
+        v_codes = {}
 
-        def gather(lo, hi):
-            for a in range(K_PASSES):
-                nc.vector.tensor_copy(
-                    v_codes[a][:, lo:hi], table[a][:].bitcast(U32).indirect(lists[:, lo // 16 : hi // 16])
-                )
+        early = keep.tile([P, 768], U32, name="v_codes_early", align_bytes=64)
+        held = mid.tile([P, held_words], U32, name="v_codes_held", align_bytes=64, offset=0)
+
+        def gather(a, lo, hi, codes):
+            nc.vector.tensor_copy(codes, table[a][:].bitcast(U32).indirect(lists[:, lo // 16 : hi // 16]))
+            for s in range(lo // STEP, hi // STEP):
+                v_codes[a, s] = codes[:, s * STEP - lo : (s + 1) * STEP - lo]
 
         squares = {}
         speeds = {}
@@ -149,17 +161,17 @@ def tile_list_surge_gauge_monitor_kernel(
                         out=bank[:, t, :],
                         lhsT=wc_codes[b][:, a, 2 * P * t : 2 * P * (t + 1)].bitcast(FP4X4),
                         lhsT_scale=wc_planes[b][:, a, P * t : P * (t + 1)],
-                        rhs=v_codes[a][:, cols].bitcast(FP8X4),
+                        rhs=v_codes[a, s].bitcast(FP8X4),
                         rhs_scale=v_scales[a][:, cols],
                         start=(a == 0),
                         stop=(a == K_PASSES - 1),
                     )
-            square = keep.tile([P, STEP, PACK], F32, name="square%d_%d" % (b, s))
+            square = keep.tile([P, STEP, PACK], F32, name="square%d_%d" % (b, s), align_bytes=64)
             nc.scalar.activation(square[:], bank[:].rearrange("p t j -> p j t"), ACT.Square)
             squares[b, s] = square
 
         def speed(b, s):
-            root = keep.tile([P, STEP, PACK], F32, name="speed%d_%d" % (b, s))
+            root = keep.tile([P, STEP, PACK], F32, name="speed%d_%d" % (b, s), align_bytes=64)
             nc.scalar.activation(root[:], squares[b, s][:], ACT.Sqrt, bias=1.0)
             speeds[b, s] = root
 
@@ -167,28 +179,32 @@ def tile_list_surge_gauge_monitor_kernel(
         wf_planes = {}
         wf_round = {}
 
-        def round_wf(b, a, copy):
-            rounded = keep.tile([P, PACK, P, PACK], BF16, name="wf_round%d%d" % (b, a), align_bytes=64)
-            copy(
-                rounded[:].rearrange("p t m i -> p m i t"),
-                wf_raw[b, a].rearrange("p i (m t) -> p m i t", t=PACK),
-            )
-            wf_round[b, a] = rounded
+        def round_wf(b, slot, on_scalar):
+            rounded = keep.tile([P, K_PASSES, PACK, P, PACK], BF16, name="wf_round%d" % b, tag=slot, align_bytes=64)
+            for a in range(K_PASSES):
+                target = rounded[:, a].rearrange("p t m i -> p m t i")
+                source = wf_raw[b, a].rearrange("p i (m t) -> p m t i", t=PACK)
+                if on_scalar[a] > 0:
+                    nc.scalar.copy(target[:, : on_scalar[a]], source[:, : on_scalar[a]])
+                if on_scalar[a] < P:
+                    nc.vector.tensor_copy(target[:, on_scalar[a] :], source[:, on_scalar[a] :])
+            wf_round[b] = rounded
 
-        def quantise_wf(b, a):
-            codes = keep.tile([P, PASS], U32, name="wf_codes%d%d" % (b, a), align_bytes=64)
-            plane = keep.tile([P, PASS], U8, name="wf_plane%d%d" % (b, a), align_bytes=64)
+        def quantise_wf(b, slot):
+            codes = keep.tile([P, K_PASSES * PASS], U32, name="wf_codes%d" % b, tag=slot, align_bytes=64)
+            plane = keep.tile([P, K_PASSES * PASS], U8, name="wf_plane%d" % b, align_bytes=64)
             nc.vector.quantize_mx(
                 out=codes[:].bitcast(FP8X4),
                 scales=plane[:],
-                in_=wf_round[b, a][:].rearrange("p t m i -> p (t m i)"),
+                in_=wf_round[b][:].rearrange("p a t m i -> p (a t m i)"),
             )
-            wf_codes[b, a] = codes
-            wf_planes[b, a] = plane
+            for a in range(K_PASSES):
+                wf_codes[b, a] = codes[:, a * PASS : (a + 1) * PASS]
+                wf_planes[b, a] = plane[:, a * PASS : (a + 1) * PASS]
 
-        drags = {}
-        h_codes = {}
-        h_planes = {}
+        drags = [keep.tile([P, S, PACK], BF16, name="drag%d" % b, align_bytes=64) for b in range(R_PASSES)]
+        h_codes = [keep.tile([P, S], U32, name="h_codes%d" % b, align_bytes=64) for b in range(R_PASSES)]
+        h_planes = [keep.tile([P, S], U8, name="h_planes%d" % b, align_bytes=64) for b in range(R_PASSES)]
 
         def drag(b, s):
             cols = slice(s * STEP, (s + 1) * STEP)
@@ -199,76 +215,88 @@ def tile_list_surge_gauge_monitor_kernel(
                         out=bank[:, t, :],
                         lhsT=wf_codes[b, a][:, P * t : P * (t + 1)].bitcast(FP8X4),
                         lhsT_scale=wf_planes[b, a][:, P * t : P * (t + 1)],
-                        rhs=v_codes[a][:, cols].bitcast(FP8X4),
+                        rhs=v_codes[a, s].bitcast(FP8X4),
                         rhs_scale=v_scales[a][:, cols],
                         start=(a == 0),
                         stop=(a == K_PASSES - 1),
                     )
-            h = keep.tile([P, STEP, PACK], BF16, name="drag%d_%d" % (b, s), align_bytes=64)
-            nc.vector.tensor_tensor(h[:], bank[:].rearrange("p t j -> p j t"), speeds[b, s][:], ALU.mult)
-            drags[b, s] = h
+            nc.vector.tensor_tensor(drags[b][:, cols, :], bank[:].rearrange("p t j -> p j t"), speeds[b, s][:], ALU.mult)
 
-        def quantise_drag(b, s):
-            codes = keep.tile([P, STEP], U32, name="h_codes%d_%d" % (b, s), align_bytes=64)
-            plane = keep.tile([P, STEP], U8, name="h_plane%d_%d" % (b, s), align_bytes=64)
+        def quantise_drag(b, lo, hi):
+            cols = slice(lo * STEP, hi * STEP)
             nc.vector.quantize_mx(
-                out=codes[:].bitcast(FP8X4), scales=plane[:], in_=drags[b, s][:].rearrange("p j t -> p (j t)")
+                out=h_codes[b][:, cols].bitcast(FP8X4),
+                scales=h_planes[b][:, cols],
+                in_=drags[b][:, cols, :].rearrange("p j t -> p (j t)"),
             )
-            h_codes[b, s] = codes
-            h_planes[b, s] = plane
 
-        def innovation(s):
-            cols = slice(s * STEP, (s + 1) * STEP)
-            bank = psum_l.tile([P, N_TILES, STEP], F32, name="level_bank")
-            for u in range(N_TILES):
-                for b in range(R_PASSES):
-                    nc.tensor.matmul_mx(
-                        out=bank[:, u, :],
-                        lhsT=wl_codes[:, b, P * u : P * (u + 1)].bitcast(FP8X4),
-                        lhsT_scale=wl_planes[:, b, P * u : P * (u + 1)],
-                        rhs=h_codes[b, s][:].bitcast(FP8X4),
-                        rhs_scale=h_planes[b, s][:],
-                        start=(b == 0),
-                        stop=(b == R_PASSES - 1),
-                    )
-            gap = ring.tile([P, N_TILES, STEP], F32, name="gap")
-            nc.vector.tensor_tensor(gap[:], observed[:, :, cols], bank[:], ALU.subtract)
-            bounded = ring.tile([P, N_TILES, STEP], F32, name="bounded")
+        def innovation(lo, hi):
+            cols = slice(lo * STEP, hi * STEP)
+            width = (hi - lo) * STEP
+            per_bank = min(N_TILES, PASS // width)
+            gap = ring.tile([P, N_TILES, width], F32, name="gap")
+            for first in range(0, N_TILES, per_bank):
+                tiles = range(first, min(first + per_bank, N_TILES))
+                bank = psum_l.tile([P, len(tiles), width], F32, name="level_bank")
+                for u in tiles:
+                    for b in range(R_PASSES):
+                        nc.tensor.matmul_mx(
+                            out=bank[:, u - first, :],
+                            lhsT=wl_codes[:, b, P * u : P * (u + 1)].bitcast(FP8X4),
+                            lhsT_scale=wl_planes[:, b, P * u : P * (u + 1)],
+                            rhs=h_codes[b][:, cols].bitcast(FP8X4),
+                            rhs_scale=h_planes[b][:, cols],
+                            start=(b == 0),
+                            stop=(b == R_PASSES - 1),
+                        )
+                rows = slice(tiles.start, tiles.stop)
+                nc.vector.tensor_tensor(gap[:, rows, :], observed[:, rows, cols], bank[:], ALU.subtract)
+            bounded = ring.tile([P, N_TILES, width], F32, name="bounded")
             nc.scalar.activation(bounded[:], gap[:], ACT.Tanh)
             nc.sync.dma_start(out.rearrange("(u p) j -> p u j", p=P)[:, :, cols], bounded[:])
 
-        gather(*GATHERS[0])
-        gather(*GATHERS[1])
-        gather(*GATHERS[2])
+        gather(0, 0, 256, early[:, :256])
+        gather(1, 0, 256, early[:, 256:512])
+        gather(1, 256, 512, early[:, 512:])
+        gather(0, 256, 512, held[:, :256])
+        gather(0, 512, S, held[:, 256:768])
+        gather(1, 512, S, held[:, 768:])
         order_wc_scales(1)
-        units = [(b, s) for b in range(R_PASSES) for s in range(STEPS)]
-        lag = 4
-        for n in range(STEPS):
-            current(*units[n])
-            if n >= lag:
-                speed(*units[n - lag])
-        round_wf(0, 0, nc.vector.tensor_copy)
-        round_wf(0, 1, nc.vector.tensor_copy)
-        quantise_wf(0, 0)
         order_wc_codes(1)
-        quantise_wf(0, 1)
-        round_wf(1, 0, nc.vector.tensor_copy)
-        round_wf(1, 1, nc.scalar.copy)
-        quantise_wf(1, 0)
+        units = [(b, s) for b in range(R_PASSES) for s in range(STEPS)]
+
+        def roots_after(n):
+            return max(0, min(len(units), n + 1 - min(5, 1 + n // 2)))
+
+        def current_and_speed(n):
+            if n < len(units):
+                current(*units[n])
+            for m in range(roots_after(n - 1), roots_after(n)):
+                speed(*units[m])
+
+        ahead = STEPS + 2
+        for n in range(ahead):
+            current_and_speed(n)
+        round_wf(0, "wf_round0", (0, 0))
+        quantise_wf(0, "wf_codes0")
         for s in range(STEPS):
-            current(1, s)
-            speed(*units[STEPS + s - lag])
+            current_and_speed(ahead + s)
             drag(0, s)
-            if s > 0:
-                quantise_drag(0, s - 1)
-        quantise_wf(1, 1)
-        quantise_drag(0, STEPS - 1)
+            if s == 1:
+                round_wf(1, "speed0_1", (0, 80))
+            if s == 4:
+                quantise_wf(1, "speed0_4")
+            if s == 5:
+                quantise_drag(0, 0, 4)
+        spans = [(0, 2), (2, 4), (4, 6), (6, 7), (7, 8)]
         for s in range(STEPS + 2):
-            if s < lag:
-                speed(1, STEPS - lag + s)
+            current_and_speed(ahead + STEPS + s)
             if s < STEPS:
                 drag(1, s)
-            if 0 < s <= STEPS:
-                quantise_drag(1, s - 1)
-            if s > 1:
-                innovation(s - 2)
+            if s == 0:
+                quantise_drag(0, 4, 8)
+            for lo, hi in spans:
+                if hi == s:
+                    quantise_drag(1, lo, hi)
+                if hi + 1 == s:
+                    innovation(lo, hi)

@@ -23,9 +23,11 @@ K_PASSES = K // PASS
 R_PASSES = H // PASS
 STEP = 128
 STEPS = S // STEP
+HALF = 512
+HALVES = S // HALF
+RUN = 4
 N_TILES = N // P
 QUADS = 4
-GATHERS = [(0, 256), (256, 512), (512, 1024)]
 
 
 def tile_list_surge_gauge_monitor_kernel(
@@ -34,6 +36,8 @@ def tile_list_surge_gauge_monitor_kernel(
     nc = tc.nc
     with ExitStack() as ctx:
         keep = ctx.enter_context(tc.tile_pool(name="keep", bufs=1))
+        late = ctx.enter_context(tc.tile_pool(name="late", bufs=1))
+        mid = ctx.enter_context(tc.tile_pool(name="mid", bufs=1))
         ring = ctx.enter_context(tc.tile_pool(name="ring", bufs=5))
         psum_a = ctx.enter_context(tc.psum_pool(name="psum_a", bufs=3))
         psum_b = ctx.enter_context(tc.psum_pool(name="psum_b", bufs=3))
@@ -44,9 +48,9 @@ def tile_list_surge_gauge_monitor_kernel(
 
         warm = keep.tile([P, 8], F32, name="warm")
         warm_out = keep.tile([P, 8], F32, name="warm_out")
-        late = ctx.enter_context(tc.tile_pool(name="late", bufs=1))
-        late_words = R_PASSES * N + R_PASSES * N // 4
-        tab_rows = late.tile([P, T], U8, name="tab_rows", offset=4 * late_words - T // 2)
+        wl_words_end = R_PASSES * N
+        packed_words = wl_words_end + R_PASSES * N // 4
+        tab_rows = late.tile([P, T], U8, name="tab_rows", offset=4 * packed_words - T // 2)
         wc_rows = keep.tile([P, K_PASSES, H], U8, name="wc_rows")
         v_scales = [keep.tile([P, S], U8, name="v_scales%d" % a, align_bytes=64) for a in range(K_PASSES)]
         nc.gpsimd.memset(tab_rows[:].bitcast(I32), 0)
@@ -56,12 +60,13 @@ def tile_list_surge_gauge_monitor_kernel(
         nc.vector.memset(v_scales[1][:].bitcast(I32), 0)
 
         wc_hbm = wc_words.rearrange("a p c -> p a c").bitcast(I32)
-        wc_raw = [keep.tile([P, PASS], I32, name="wc_raw%d" % b) for b in range(R_PASSES)]
+        wc_raw = [keep.tile([P, PASS], I32, name="wc_raw%d" % b)[:] for b in range(R_PASSES)]
         table = [keep.tile([P, T], I32, name="table%d" % a) for a in range(K_PASSES)]
+        wf_raw = {}
 
         def load_wc(b):
             nc.sync.dma_start(
-                wc_raw[b][:].rearrange("p (a c) -> p a c", a=K_PASSES),
+                wc_raw[b].rearrange("p (a c) -> p a c", a=K_PASSES),
                 wc_hbm[:, :, b * PASS // 2 : (b + 1) * PASS // 2],
             )
 
@@ -75,6 +80,12 @@ def tile_list_surge_gauge_monitor_kernel(
                     rows[:, 4 * d : 4 * d + 4, :].rearrange("a q c -> q a c").bitcast(I32),
                 )
 
+        def load_wf(b, a):
+            nc.sync.dma_start(
+                wf_raw[b, a].rearrange("p (i c) -> p i c", i=PACK),
+                wf[a * PASS : (a + 1) * PASS, b * PASS : (b + 1) * PASS].rearrange("(p i) c -> p i c", i=PACK),
+            )
+
         load_wc(0)
         for e in range(2):
             nc.sync.dma_start(tab_rows[e:P:16, :].bitcast(I32), tab_scales[0, e::2, :].bitcast(I32))
@@ -85,13 +96,12 @@ def tile_list_surge_gauge_monitor_kernel(
         load_table(1)
 
         wc_codes = {0: keep.tile([P, K_PASSES, 2 * PASS], U8, name="wc_codes0", align_bytes=64)[:]}
-        mid = ctx.enter_context(tc.tile_pool(name="mid", bufs=1))
         wc_planes = {0: keep.tile([P, K_PASSES, PASS], U8, name="wc_planes0", align_bytes=64)[:]}
 
         def order_wc_codes(b):
             nc.vector.tensor_copy(
                 wc_codes[b].bitcast(U16).rearrange("p a (t m) -> p a t m", t=PACK),
-                wc_raw[b][:].bitcast(U16).rearrange("p (a m t) -> p a t m", a=K_PASSES, t=PACK),
+                wc_raw[b].bitcast(U16).rearrange("p (a m t) -> p a t m", a=K_PASSES, t=PACK),
             )
 
         def order_wc_scales(b):
@@ -101,8 +111,7 @@ def tile_list_surge_gauge_monitor_kernel(
             )
 
         order_wc_codes(0)
-        held_words = 1280
-        picked_rows = mid.tile([P, S], U8, name="picked_rows", offset=4 * held_words - S // 2, align_bytes=64)
+        picked_rows = mid.tile([P, S], U8, name="picked_rows", offset=4 * HALF - S // 2, align_bytes=64)
         nc.vector.tensor_copy(picked_rows[:], tab_rows[:].indirect(lists[:]))
         picked = picked_rows[:].bitcast(I32)
         nc.vector.tensor_copy(v_scales[0][:].bitcast(I32), picked)
@@ -110,85 +119,76 @@ def tile_list_surge_gauge_monitor_kernel(
             nc.sync.dma_start(v_scales[1][r:P:32, :].bitcast(I32), picked[8 * r + 2 : P : 32, :])
         for e in range(2):
             nc.sync.dma_start(v_scales[0][2 + e : P : 32, :].bitcast(I32), picked[16 + e : P : 32, :])
-
-        packed = late.tile([P, late_words], I32, name="packed", offset=0, align_bytes=64)
         order_wc_scales(0)
-        floats = late.tile([P, R_PASSES * K_PASSES * PACK * PASS + N_TILES * S], F32, name="floats", offset=4 * late_words)
-        wf_raw = {}
 
-        def load_wf(b, a):
-            first = (b * K_PASSES + a) * PACK * PASS
-            raw = floats[:, first : first + PACK * PASS].rearrange("p (i c) -> p i c", i=PACK)
-            nc.sync.dma_start(
-                raw, wf[a * PASS : (a + 1) * PASS, b * PASS : (b + 1) * PASS].rearrange("(p i) c -> p i c", i=PACK)
-            )
-            wf_raw[b, a] = raw
-
-        load_wf(0, 0)
-        load_wf(0, 1)
-        load_wf(1, 0)
-        load_wf(1, 1)
-        wl_codes = packed[:, : R_PASSES * N].rearrange("p (b c) -> p b c", b=R_PASSES)
+        chunk = PACK * PASS
+        packed = late.tile([P, packed_words], I32, name="packed", offset=0, align_bytes=64)
+        floats = late.tile([P, 4 * chunk + N_TILES * S], F32, name="floats", offset=4 * packed_words)
+        for b in range(R_PASSES):
+            for a in range(K_PASSES):
+                first = (b * K_PASSES + a) * chunk
+                wf_raw[b, a] = floats[:, first : first + chunk]
+                load_wf(b, a)
+        wl_codes = packed[:, :wl_words_end].rearrange("p (b c) -> p b c", b=R_PASSES)
         nc.sync.dma_start(wl_codes, wl_words.rearrange("a p c i -> p a (c i)").bitcast(I32))
-        nc.gpsimd.memset(packed[:, R_PASSES * N :], 0)
-        wl_planes = packed[:, R_PASSES * N :].bitcast(U8).rearrange("p (b c) -> p b c", b=R_PASSES)
+        nc.gpsimd.memset(packed[:, wl_words_end:], 0)
+        wl_planes = packed[:, wl_words_end:].bitcast(U8).rearrange("p (b c) -> p b c", b=R_PASSES)
         load_planes(wl_planes, wl_scales)
-        observed = floats[:, R_PASSES * K_PASSES * PACK * PASS :].rearrange("p (u j) -> p u j", u=N_TILES)
+        observed = floats[:, 4 * chunk :].rearrange("p (u j) -> p u j", u=N_TILES)
         nc.sync.dma_start(observed, obs.rearrange("(u p) j -> p u j", p=P))
 
-        wc_second = mid.tile([P, 3 * K_PASSES * PASS], U8, name="wc_second", align_bytes=64, offset=4 * held_words)
+        wc_second = mid.tile([P, 3 * K_PASSES * PASS], U8, name="wc_second", offset=4 * HALF, align_bytes=64)
         wc_codes[1] = wc_second[:, : 2 * K_PASSES * PASS].rearrange("p (a c) -> p a c", a=K_PASSES)
         wc_planes[1] = wc_second[:, 2 * K_PASSES * PASS :].rearrange("p (a c) -> p a c", a=K_PASSES)
-        v_codes = {}
 
-        early = keep.tile([P, 768], U32, name="v_codes_early", align_bytes=64)
-        held = mid.tile([P, held_words], U32, name="v_codes_held", align_bytes=64, offset=0)
+        v_codes = {
+            (0, 0): keep.tile([P, HALF], U32, name="v_codes00", align_bytes=64),
+            (1, 0): keep.tile([P, HALF], U32, name="v_codes10", align_bytes=64),
+            (1, 1): keep.tile([P, HALF], U32, name="v_codes11", align_bytes=64),
+            (0, 1): mid.tile([P, HALF], U32, name="v_codes01", offset=0, align_bytes=64),
+        }
 
-        def gather(a, lo, hi, codes):
-            nc.vector.tensor_copy(codes, table[a][:].bitcast(U32).indirect(lists[:, lo // 16 : hi // 16]))
-            for s in range(lo // STEP, hi // STEP):
-                v_codes[a, s] = codes[:, s * STEP - lo : (s + 1) * STEP - lo]
+        def gather(a, h):
+            nc.vector.tensor_copy(
+                v_codes[a, h][:], table[a][:].bitcast(U32).indirect(lists[:, h * HALF // 16 : (h + 1) * HALF // 16])
+            )
 
-        squares = {}
+        squares = {
+            (b, h): keep.tile([P, HALF // RUN, PACK, RUN], F32, name="square%d_%d" % (b, h))
+            for b in range(R_PASSES)
+            for h in range(HALVES)
+        }
         speeds = {}
 
-        def current(b, s):
-            cols = slice(s * STEP, (s + 1) * STEP)
-            bank = psum_a.tile([P, PACK, STEP], F32, name="a_bank")
-            for t in range(PACK):
-                for a in range(K_PASSES):
-                    nc.tensor.matmul_mx(
-                        out=bank[:, t, :],
-                        lhsT=wc_codes[b][:, a, 2 * P * t : 2 * P * (t + 1)].bitcast(FP4X4),
-                        lhsT_scale=wc_planes[b][:, a, P * t : P * (t + 1)],
-                        rhs=v_codes[a, s].bitcast(FP8X4),
-                        rhs_scale=v_scales[a][:, cols],
-                        start=(a == 0),
-                        stop=(a == K_PASSES - 1),
-                    )
-            square = keep.tile([P, STEP, PACK], F32, name="square%d_%d" % (b, s), align_bytes=64)
-            nc.scalar.activation(square[:], bank[:].rearrange("p t j -> p j t"), ACT.Square)
-            squares[b, s] = square
+        def current(b, h, t):
+            bank = psum_a.tile([P, HALF], F32, name="a_bank")
+            for a in range(K_PASSES):
+                nc.tensor.matmul_mx(
+                    out=bank[:],
+                    lhsT=wc_codes[b][:, a, 2 * P * t : 2 * P * (t + 1)].bitcast(FP4X4),
+                    lhsT_scale=wc_planes[b][:, a, P * t : P * (t + 1)],
+                    rhs=v_codes[a, h][:].bitcast(FP8X4),
+                    rhs_scale=v_scales[a][:, h * HALF : (h + 1) * HALF],
+                    start=(a == 0),
+                    stop=(a == K_PASSES - 1),
+                )
+            nc.scalar.activation(squares[b, h][:, :, t, :], bank[:].rearrange("p (c i) -> p c i", i=RUN), ACT.Square)
 
         def speed(b, s):
-            root = keep.tile([P, STEP, PACK], F32, name="speed%d_%d" % (b, s), align_bytes=64)
-            nc.scalar.activation(root[:], squares[b, s][:], ACT.Sqrt, bias=1.0)
+            h, first = divmod(s * STEP, HALF)
+            root = keep.tile([P, STEP // RUN, PACK, RUN], F32, name="speed%d_%d" % (b, s), align_bytes=64)
+            nc.scalar.activation(root[:], squares[b, h][:, first // RUN : (first + STEP) // RUN], ACT.Sqrt, bias=1.0)
             speeds[b, s] = root
 
         wf_codes = {}
         wf_planes = {}
         wf_round = {}
 
-        def round_wf(b, slot, on_scalar):
-            rounded = keep.tile([P, K_PASSES, PACK, P, PACK], BF16, name="wf_round%d" % b, tag=slot, align_bytes=64)
-            for a in range(K_PASSES):
-                target = rounded[:, a].rearrange("p t m i -> p m t i")
-                source = wf_raw[b, a].rearrange("p i (m t) -> p m t i", t=PACK)
-                if on_scalar[a] > 0:
-                    nc.scalar.copy(target[:, : on_scalar[a]], source[:, : on_scalar[a]])
-                if on_scalar[a] < P:
-                    nc.vector.tensor_copy(target[:, on_scalar[a] :], source[:, on_scalar[a] :])
-            wf_round[b] = rounded
+        def round_wf(b, a, copy):
+            copy(
+                wf_round[b][:, a].rearrange("p t m i -> p m i t"),
+                wf_raw[b, a].rearrange("p (i m t) -> p m i t", i=PACK, t=PACK),
+            )
 
         def quantise_wf(b, slot):
             codes = keep.tile([P, K_PASSES * PASS], U32, name="wf_codes%d" % b, tag=slot, align_bytes=64)
@@ -208,6 +208,7 @@ def tile_list_surge_gauge_monitor_kernel(
 
         def drag(b, s):
             cols = slice(s * STEP, (s + 1) * STEP)
+            h, first = divmod(s * STEP, HALF)
             bank = psum_b.tile([P, PACK, STEP], F32, name="b_bank")
             for t in range(PACK):
                 for a in range(K_PASSES):
@@ -215,12 +216,17 @@ def tile_list_surge_gauge_monitor_kernel(
                         out=bank[:, t, :],
                         lhsT=wf_codes[b, a][:, P * t : P * (t + 1)].bitcast(FP8X4),
                         lhsT_scale=wf_planes[b, a][:, P * t : P * (t + 1)],
-                        rhs=v_codes[a, s].bitcast(FP8X4),
+                        rhs=v_codes[a, h][:, first : first + STEP].bitcast(FP8X4),
                         rhs_scale=v_scales[a][:, cols],
                         start=(a == 0),
                         stop=(a == K_PASSES - 1),
                     )
-            nc.vector.tensor_tensor(drags[b][:, cols, :], bank[:].rearrange("p t j -> p j t"), speeds[b, s][:], ALU.mult)
+            nc.vector.tensor_tensor(
+                drags[b][:, cols, :].rearrange("p (c i) t -> p c t i", i=RUN),
+                bank[:].rearrange("p t (c i) -> p c t i", i=RUN),
+                speeds[b, s][:],
+                ALU.mult,
+            )
 
         def quantise_drag(b, lo, hi):
             cols = slice(lo * STEP, hi * STEP)
@@ -255,42 +261,43 @@ def tile_list_surge_gauge_monitor_kernel(
             nc.scalar.activation(bounded[:], gap[:], ACT.Tanh)
             nc.sync.dma_start(out.rearrange("(u p) j -> p u j", p=P)[:, :, cols], bounded[:])
 
-        gather(0, 0, 256, early[:, :256])
-        gather(1, 0, 256, early[:, 256:512])
-        gather(1, 256, 512, early[:, 512:])
-        gather(0, 256, 512, held[:, :256])
-        gather(0, 512, S, held[:, 256:768])
-        gather(1, 512, S, held[:, 768:])
+        gather(0, 0)
+        gather(1, 0)
+        gather(1, 1)
+        gather(0, 1)
         order_wc_scales(1)
-        order_wc_codes(1)
-        units = [(b, s) for b in range(R_PASSES) for s in range(STEPS)]
-
-        def roots_after(n):
-            return max(0, min(len(units), n + 1 - min(5, 1 + n // 2)))
+        banks = [(b, h, t) for b in range(R_PASSES) for h in range(HALVES) for t in range(PACK)]
+        steps = [(b, s) for b in range(R_PASSES) for s in range(STEPS)]
 
         def current_and_speed(n):
-            if n < len(units):
-                current(*units[n])
-            for m in range(roots_after(n - 1), roots_after(n)):
-                speed(*units[m])
+            if n < len(banks):
+                current(*banks[n])
+            if PACK <= n < len(steps) + PACK:
+                speed(*steps[n - PACK])
 
-        ahead = STEPS + 2
-        for n in range(ahead):
+        for n in range(STEPS):
             current_and_speed(n)
-        round_wf(0, "wf_round0", (0, 0))
+        wf_round[0] = keep.tile([P, K_PASSES, PACK, P, PACK], BF16, name="wf_round0", align_bytes=64)
+        round_wf(0, 0, nc.vector.tensor_copy)
+        order_wc_codes(1)
+        round_wf(0, 1, nc.vector.tensor_copy)
         quantise_wf(0, "wf_codes0")
         for s in range(STEPS):
-            current_and_speed(ahead + s)
+            current_and_speed(STEPS + s)
             drag(0, s)
             if s == 1:
-                round_wf(1, "speed0_1", (0, 80))
+                wf_round[1] = keep.tile(
+                    [P, K_PASSES, PACK, P, PACK], BF16, name="wf_round1", tag="speed0_1", align_bytes=64
+                )
+                round_wf(1, 0, nc.vector.tensor_copy)
+                round_wf(1, 1, nc.scalar.copy)
             if s == 4:
                 quantise_wf(1, "speed0_4")
             if s == 5:
                 quantise_drag(0, 0, 4)
         spans = [(0, 2), (2, 4), (4, 6), (6, 7), (7, 8)]
         for s in range(STEPS + 2):
-            current_and_speed(ahead + STEPS + s)
+            current_and_speed(2 * STEPS + s)
             if s < STEPS:
                 drag(1, s)
             if s == 0:

@@ -20,14 +20,18 @@ P = 128
 PACK = 4
 PASS = P * PACK
 K_PASSES = K // PASS
-R_PASSES = H // PASS
-STEP = 128
-STEPS = S // STEP
+R_BLOCKS = H // PASS
+QUADRANT = 32
+PLANE_ROWS = 4
+GROUP = 16
 HALF = 512
 HALVES = S // HALF
+STEP = 128
+STEPS = S // STEP
 RUN = 4
 N_TILES = N // P
-QUADS = 4
+SPANS = [(0, 2), (2, 4), (4, 6), (6, 7), (7, 8)]
+ROUND_AFTER, QUANTISE_WF_AFTER, QUANTISE_H_AFTER = 1, 4, 5
 
 
 def tile_list_surge_gauge_monitor_kernel(
@@ -38,109 +42,109 @@ def tile_list_surge_gauge_monitor_kernel(
         keep = ctx.enter_context(tc.tile_pool(name="keep", bufs=1))
         late = ctx.enter_context(tc.tile_pool(name="late", bufs=1))
         mid = ctx.enter_context(tc.tile_pool(name="mid", bufs=1))
-        ring = ctx.enter_context(tc.tile_pool(name="ring", bufs=5))
-        psum_a = ctx.enter_context(tc.psum_pool(name="psum_a", bufs=3))
-        psum_b = ctx.enter_context(tc.psum_pool(name="psum_b", bufs=3))
-        psum_l = ctx.enter_context(tc.psum_pool(name="psum_l", bufs=2))
+        ring = ctx.enter_context(tc.tile_pool(name="ring", bufs=len(SPANS)))
+        psum_current = ctx.enter_context(tc.psum_pool(name="psum_current", bufs=3))
+        psum_flow = ctx.enter_context(tc.psum_pool(name="psum_flow", bufs=3))
+        psum_level = ctx.enter_context(tc.psum_pool(name="psum_level", bufs=2))
 
-        lists = keep.tile([P, S // 16], U16, name="lists")
+        lists = keep.tile([P, S // GROUP], U16, name="lists")
         nc.sync.dma_start(lists[:], offs)
 
-        warm = keep.tile([P, 8], F32, name="warm")
-        warm_out = keep.tile([P, 8], F32, name="warm_out")
-        wl_words_end = R_PASSES * N
-        packed_words = wl_words_end + R_PASSES * N // 4
+        one = keep.tile([P, 8], F32, name="one")
+        background = keep.tile([P, 8], F32, name="background")
+        wl_words_end = R_BLOCKS * N
+        packed_words = wl_words_end + R_BLOCKS * N // 4
         tab_rows = late.tile([P, T], U8, name="tab_rows", offset=4 * packed_words - T // 2)
         wc_rows = keep.tile([P, K_PASSES, H], U8, name="wc_rows")
-        v_scales = [keep.tile([P, S], U8, name="v_scales%d" % a, align_bytes=64) for a in range(K_PASSES)]
+        v_planes = [keep.tile([P, S], U8, name="v_plane%d" % g, align_bytes=64) for g in range(K_PASSES)]
         nc.gpsimd.memset(tab_rows[:].bitcast(I32), 0)
         nc.vector.memset(wc_rows[:].bitcast(I32), 0)
-        nc.vector.memset(warm[:], 1.0)
-        nc.scalar.activation(warm_out[:], warm[:], ACT.Sqrt, bias=1.0)
-        nc.vector.memset(v_scales[1][:].bitcast(I32), 0)
+        nc.vector.memset(one[:], 1.0)
+        nc.scalar.activation(background[:], one[:], ACT.Sqrt)
+        nc.vector.memset(v_planes[1][:].bitcast(I32), 0)
 
-        wc_hbm = wc_words.rearrange("a p c -> p a c").bitcast(I32)
-        wc_raw = [keep.tile([P, PASS], I32, name="wc_raw%d" % b)[:] for b in range(R_PASSES)]
-        table = [keep.tile([P, T], I32, name="table%d" % a) for a in range(K_PASSES)]
+        wc_hbm = wc_words.rearrange("g p c -> p g c").bitcast(I32)
+        wc_raw = [keep.tile([P, PASS], I32, name="wc_raw%d" % b)[:] for b in range(R_BLOCKS)]
+        table = [keep.tile([P, T], I32, name="table%d" % g) for g in range(K_PASSES)]
         wf_raw = {}
 
         def load_wc(b):
             nc.sync.dma_start(
-                wc_raw[b].rearrange("p (a c) -> p a c", a=K_PASSES),
+                wc_raw[b].rearrange("p (g c) -> p g c", g=K_PASSES),
                 wc_hbm[:, :, b * PASS // 2 : (b + 1) * PASS // 2],
             )
 
-        def load_table(a):
-            nc.sync.dma_start(table[a][:], tab_words[a].rearrange("p t i -> p (t i)").bitcast(I32))
+        def load_table(g):
+            nc.sync.dma_start(table[g][:], tab_words[g].rearrange("p t i -> p (t i)").bitcast(I32))
 
-        def load_planes(planes, rows):
-            for d in range(QUADS):
+        def load_planes(planes, scales):
+            for e in range(PLANE_ROWS):
                 nc.sync.dma_start(
-                    planes[32 * d : 32 * d + 4].bitcast(I32),
-                    rows[:, 4 * d : 4 * d + 4, :].rearrange("a q c -> q a c").bitcast(I32),
+                    planes[e:P:QUADRANT].bitcast(I32),
+                    scales[:, e::PLANE_ROWS, :].rearrange("g d c -> d g c").bitcast(I32),
                 )
 
-        def load_wf(b, a):
+        def load_wf(b, g):
             nc.sync.dma_start(
-                wf_raw[b, a].rearrange("p (i c) -> p i c", i=PACK),
-                wf[a * PASS : (a + 1) * PASS, b * PASS : (b + 1) * PASS].rearrange("(p i) c -> p i c", i=PACK),
+                wf_raw[b, g].rearrange("p (i c) -> p i c", i=PACK),
+                wf[g * PASS : (g + 1) * PASS, b * PASS : (b + 1) * PASS].rearrange("(p i) c -> p i c", i=PACK),
             )
 
         load_wc(0)
         for e in range(2):
-            nc.sync.dma_start(tab_rows[e:P:16, :].bitcast(I32), tab_scales[0, e::2, :].bitcast(I32))
+            nc.sync.dma_start(tab_rows[e:P:GROUP, :].bitcast(I32), tab_scales[0, e::2, :].bitcast(I32))
         nc.sync.dma_start(tab_rows[2:P:8, :].bitcast(I32), tab_scales[1].bitcast(I32))
         load_table(0)
         load_planes(wc_rows, wc_scales)
-        load_wc(1)
         load_table(1)
+        load_wc(1)
 
         wc_codes = {0: keep.tile([P, K_PASSES, 2 * PASS], U8, name="wc_codes0", align_bytes=64)[:]}
         wc_planes = {0: keep.tile([P, K_PASSES, PASS], U8, name="wc_planes0", align_bytes=64)[:]}
 
         def order_wc_codes(b):
             nc.vector.tensor_copy(
-                wc_codes[b].bitcast(U16).rearrange("p a (t m) -> p a t m", t=PACK),
-                wc_raw[b].bitcast(U16).rearrange("p (a m t) -> p a t m", a=K_PASSES, t=PACK),
+                wc_codes[b].bitcast(U16).rearrange("p g (t m) -> p g t m", t=PACK),
+                wc_raw[b].bitcast(U16).rearrange("p (g m t) -> p g t m", g=K_PASSES, t=PACK),
             )
 
-        def order_wc_scales(b):
+        def order_wc_planes(b):
             nc.vector.tensor_copy(
-                wc_planes[b].rearrange("p a (t m) -> p a t m", t=PACK),
-                wc_rows[:, :, b * PASS : (b + 1) * PASS].rearrange("p a (m t) -> p a t m", t=PACK),
+                wc_planes[b].rearrange("p g (t m) -> p g t m", t=PACK),
+                wc_rows[:, :, b * PASS : (b + 1) * PASS].rearrange("p g (m t) -> p g t m", t=PACK),
             )
 
         order_wc_codes(0)
         picked_rows = mid.tile([P, S], U8, name="picked_rows", offset=4 * HALF - S // 2, align_bytes=64)
         nc.vector.tensor_copy(picked_rows[:], tab_rows[:].indirect(lists[:]))
         picked = picked_rows[:].bitcast(I32)
-        nc.vector.tensor_copy(v_scales[0][:].bitcast(I32), picked)
-        for r in range(4):
-            nc.sync.dma_start(v_scales[1][r:P:32, :].bitcast(I32), picked[8 * r + 2 : P : 32, :])
+        nc.vector.tensor_copy(v_planes[0][:].bitcast(I32), picked)
+        for e in range(PLANE_ROWS):
+            nc.sync.dma_start(v_planes[1][e:P:QUADRANT, :].bitcast(I32), picked[8 * e + 2 : P : QUADRANT, :])
         for e in range(2):
-            nc.sync.dma_start(v_scales[0][2 + e : P : 32, :].bitcast(I32), picked[16 + e : P : 32, :])
-        order_wc_scales(0)
+            nc.sync.dma_start(v_planes[0][2 + e : P : QUADRANT, :].bitcast(I32), picked[GROUP + e : P : QUADRANT, :])
+        order_wc_planes(0)
 
-        chunk = PACK * PASS
+        piece = PACK * PASS
+        pieces = R_BLOCKS * K_PASSES
         packed = late.tile([P, packed_words], I32, name="packed", offset=0, align_bytes=64)
-        floats = late.tile([P, 4 * chunk + N_TILES * S], F32, name="floats", offset=4 * packed_words)
-        for b in range(R_PASSES):
-            for a in range(K_PASSES):
-                first = (b * K_PASSES + a) * chunk
-                wf_raw[b, a] = floats[:, first : first + chunk]
-                load_wf(b, a)
-        wl_codes = packed[:, :wl_words_end].rearrange("p (b c) -> p b c", b=R_PASSES)
-        nc.sync.dma_start(wl_codes, wl_words.rearrange("a p c i -> p a (c i)").bitcast(I32))
+        floats = late.tile([P, pieces * piece + N_TILES * S], F32, name="floats", offset=4 * packed_words)
+        for b in range(R_BLOCKS):
+            for g in range(K_PASSES):
+                first = (b * K_PASSES + g) * piece
+                wf_raw[b, g] = floats[:, first : first + piece]
+                load_wf(b, g)
+        wl_codes = packed[:, :wl_words_end].rearrange("p (b c) -> p b c", b=R_BLOCKS)
+        nc.sync.dma_start(wl_codes, wl_words.rearrange("b p c i -> p b (c i)").bitcast(I32))
         nc.gpsimd.memset(packed[:, wl_words_end:], 0)
-        wl_planes = packed[:, wl_words_end:].bitcast(U8).rearrange("p (b c) -> p b c", b=R_PASSES)
+        wl_planes = packed[:, wl_words_end:].bitcast(U8).rearrange("p (b c) -> p b c", b=R_BLOCKS)
         load_planes(wl_planes, wl_scales)
-        observed = floats[:, 4 * chunk :].rearrange("p (u j) -> p u j", u=N_TILES)
+        observed = floats[:, pieces * piece :].rearrange("p (u j) -> p u j", u=N_TILES)
         nc.sync.dma_start(observed, obs.rearrange("(u p) j -> p u j", p=P))
 
         wc_second = mid.tile([P, 3 * K_PASSES * PASS], U8, name="wc_second", offset=4 * HALF, align_bytes=64)
-        wc_codes[1] = wc_second[:, : 2 * K_PASSES * PASS].rearrange("p (a c) -> p a c", a=K_PASSES)
-        wc_planes[1] = wc_second[:, 2 * K_PASSES * PASS :].rearrange("p (a c) -> p a c", a=K_PASSES)
-
+        wc_codes[1] = wc_second[:, : 2 * K_PASSES * PASS].rearrange("p (g c) -> p g c", g=K_PASSES)
+        wc_planes[1] = wc_second[:, 2 * K_PASSES * PASS :].rearrange("p (g c) -> p g c", g=K_PASSES)
         v_codes = {
             (0, 0): keep.tile([P, HALF], U32, name="v_codes00", align_bytes=64),
             (1, 0): keep.tile([P, HALF], U32, name="v_codes10", align_bytes=64),
@@ -148,126 +152,130 @@ def tile_list_surge_gauge_monitor_kernel(
             (0, 1): mid.tile([P, HALF], U32, name="v_codes01", offset=0, align_bytes=64),
         }
 
-        def gather(a, h):
-            nc.vector.tensor_copy(
-                v_codes[a, h][:], table[a][:].bitcast(U32).indirect(lists[:, h * HALF // 16 : (h + 1) * HALF // 16])
-            )
+        def gather(g, half):
+            entries = lists[:, half * HALF // GROUP : (half + 1) * HALF // GROUP]
+            nc.vector.tensor_copy(v_codes[g, half][:], table[g][:].bitcast(U32).indirect(entries))
 
         squares = {
-            (b, h): keep.tile([P, HALF // RUN, PACK, RUN], F32, name="square%d_%d" % (b, h))
-            for b in range(R_PASSES)
-            for h in range(HALVES)
+            (b, half): keep.tile([P, HALF // RUN, PACK, RUN], F32, name="square%d_%d" % (b, half))
+            for b in range(R_BLOCKS)
+            for half in range(HALVES)
         }
         speeds = {}
 
-        def current(b, h, t):
-            bank = psum_a.tile([P, HALF], F32, name="a_bank")
-            for a in range(K_PASSES):
+        def current(b, half, t):
+            bank = psum_current.tile([P, HALF], F32, name="current_bank")
+            for g in range(K_PASSES):
                 nc.tensor.matmul_mx(
                     out=bank[:],
-                    lhsT=wc_codes[b][:, a, 2 * P * t : 2 * P * (t + 1)].bitcast(FP4X4),
-                    lhsT_scale=wc_planes[b][:, a, P * t : P * (t + 1)],
-                    rhs=v_codes[a, h][:].bitcast(FP8X4),
-                    rhs_scale=v_scales[a][:, h * HALF : (h + 1) * HALF],
-                    start=(a == 0),
-                    stop=(a == K_PASSES - 1),
+                    lhsT=wc_codes[b][:, g, 2 * P * t : 2 * P * (t + 1)].bitcast(FP4X4),
+                    lhsT_scale=wc_planes[b][:, g, P * t : P * (t + 1)],
+                    rhs=v_codes[g, half][:].bitcast(FP8X4),
+                    rhs_scale=v_planes[g][:, half * HALF : (half + 1) * HALF],
+                    start=(g == 0),
+                    stop=(g == K_PASSES - 1),
                 )
-            nc.scalar.activation(squares[b, h][:, :, t, :], bank[:].rearrange("p (c i) -> p c i", i=RUN), ACT.Square)
+            nc.scalar.activation(
+                squares[b, half][:, :, t, :], bank[:].rearrange("p (c i) -> p c i", i=RUN), ACT.Square
+            )
 
         def speed(b, s):
-            h, first = divmod(s * STEP, HALF)
+            half, first = divmod(s * STEP, HALF)
             root = keep.tile([P, STEP // RUN, PACK, RUN], F32, name="speed%d_%d" % (b, s), align_bytes=64)
-            nc.scalar.activation(root[:], squares[b, h][:, first // RUN : (first + STEP) // RUN], ACT.Sqrt, bias=1.0)
+            nc.scalar.activation(
+                root[:], squares[b, half][:, first // RUN : (first + STEP) // RUN], ACT.Sqrt, bias=background[:, :1]
+            )
             speeds[b, s] = root
 
         wf_codes = {}
         wf_planes = {}
         wf_round = {}
 
-        def round_wf(b, a, copy):
+        def round_wf(b, g, copy):
             copy(
-                wf_round[b][:, a].rearrange("p t m i -> p m i t"),
-                wf_raw[b, a].rearrange("p (i m t) -> p m i t", i=PACK, t=PACK),
+                wf_round[b][:, g].rearrange("p t m i -> p m i t"),
+                wf_raw[b, g].rearrange("p (i m t) -> p m i t", i=PACK, t=PACK),
             )
 
-        def quantise_wf(b, slot):
-            codes = keep.tile([P, K_PASSES * PASS], U32, name="wf_codes%d" % b, tag=slot, align_bytes=64)
-            plane = keep.tile([P, K_PASSES * PASS], U8, name="wf_plane%d" % b, align_bytes=64)
+        def quantise_wf(b, tag):
+            codes = keep.tile([P, K_PASSES * PASS], U32, name="wf_codes%d" % b, tag=tag, align_bytes=64)
+            planes = keep.tile([P, K_PASSES * PASS], U8, name="wf_planes%d" % b, align_bytes=64)
             nc.vector.quantize_mx(
                 out=codes[:].bitcast(FP8X4),
-                scales=plane[:],
-                in_=wf_round[b][:].rearrange("p a t m i -> p (a t m i)"),
+                scales=planes[:],
+                in_=wf_round[b][:].rearrange("p g t m i -> p (g t m i)"),
             )
-            for a in range(K_PASSES):
-                wf_codes[b, a] = codes[:, a * PASS : (a + 1) * PASS]
-                wf_planes[b, a] = plane[:, a * PASS : (a + 1) * PASS]
+            for g in range(K_PASSES):
+                wf_codes[b, g] = codes[:, g * PASS : (g + 1) * PASS]
+                wf_planes[b, g] = planes[:, g * PASS : (g + 1) * PASS]
 
-        drags = [keep.tile([P, S, PACK], BF16, name="drag%d" % b, align_bytes=64) for b in range(R_PASSES)]
-        h_codes = [keep.tile([P, S], U32, name="h_codes%d" % b, align_bytes=64) for b in range(R_PASSES)]
-        h_planes = [keep.tile([P, S], U8, name="h_planes%d" % b, align_bytes=64) for b in range(R_PASSES)]
+        drags = [keep.tile([P, S, PACK], BF16, name="drag%d" % b, align_bytes=64) for b in range(R_BLOCKS)]
+        h_codes = [keep.tile([P, S], U32, name="h_codes%d" % b, align_bytes=64) for b in range(R_BLOCKS)]
+        h_planes = [keep.tile([P, S], U8, name="h_plane%d" % b, align_bytes=64) for b in range(R_BLOCKS)]
 
         def drag(b, s):
-            cols = slice(s * STEP, (s + 1) * STEP)
-            h, first = divmod(s * STEP, HALF)
-            bank = psum_b.tile([P, PACK, STEP], F32, name="b_bank")
+            gauges = slice(s * STEP, (s + 1) * STEP)
+            half, first = divmod(s * STEP, HALF)
+            bank = psum_flow.tile([P, PACK, STEP], F32, name="flow_bank")
             for t in range(PACK):
-                for a in range(K_PASSES):
+                for g in range(K_PASSES):
                     nc.tensor.matmul_mx(
                         out=bank[:, t, :],
-                        lhsT=wf_codes[b, a][:, P * t : P * (t + 1)].bitcast(FP8X4),
-                        lhsT_scale=wf_planes[b, a][:, P * t : P * (t + 1)],
-                        rhs=v_codes[a, h][:, first : first + STEP].bitcast(FP8X4),
-                        rhs_scale=v_scales[a][:, cols],
-                        start=(a == 0),
-                        stop=(a == K_PASSES - 1),
+                        lhsT=wf_codes[b, g][:, P * t : P * (t + 1)].bitcast(FP8X4),
+                        lhsT_scale=wf_planes[b, g][:, P * t : P * (t + 1)],
+                        rhs=v_codes[g, half][:, first : first + STEP].bitcast(FP8X4),
+                        rhs_scale=v_planes[g][:, gauges],
+                        start=(g == 0),
+                        stop=(g == K_PASSES - 1),
                     )
             nc.vector.tensor_tensor(
-                drags[b][:, cols, :].rearrange("p (c i) t -> p c t i", i=RUN),
+                drags[b][:, gauges, :].rearrange("p (c i) t -> p c t i", i=RUN),
                 bank[:].rearrange("p t (c i) -> p c t i", i=RUN),
                 speeds[b, s][:],
                 ALU.mult,
             )
 
         def quantise_drag(b, lo, hi):
-            cols = slice(lo * STEP, hi * STEP)
+            gauges = slice(lo * STEP, hi * STEP)
             nc.vector.quantize_mx(
-                out=h_codes[b][:, cols].bitcast(FP8X4),
-                scales=h_planes[b][:, cols],
-                in_=drags[b][:, cols, :].rearrange("p j t -> p (j t)"),
+                out=h_codes[b][:, gauges].bitcast(FP8X4),
+                scales=h_planes[b][:, gauges],
+                in_=drags[b][:, gauges, :].rearrange("p j t -> p (j t)"),
             )
 
         def innovation(lo, hi):
-            cols = slice(lo * STEP, hi * STEP)
+            gauges = slice(lo * STEP, hi * STEP)
             width = (hi - lo) * STEP
-            per_bank = min(N_TILES, PASS // width)
+            per_bank = min(N_TILES, HALF // width)
             gap = ring.tile([P, N_TILES, width], F32, name="gap")
             for first in range(0, N_TILES, per_bank):
                 tiles = range(first, min(first + per_bank, N_TILES))
-                bank = psum_l.tile([P, len(tiles), width], F32, name="level_bank")
+                bank = psum_level.tile([P, len(tiles), width], F32, name="level_bank")
                 for u in tiles:
-                    for b in range(R_PASSES):
+                    for b in range(R_BLOCKS):
                         nc.tensor.matmul_mx(
                             out=bank[:, u - first, :],
                             lhsT=wl_codes[:, b, P * u : P * (u + 1)].bitcast(FP8X4),
                             lhsT_scale=wl_planes[:, b, P * u : P * (u + 1)],
-                            rhs=h_codes[b][:, cols].bitcast(FP8X4),
-                            rhs_scale=h_planes[b][:, cols],
+                            rhs=h_codes[b][:, gauges].bitcast(FP8X4),
+                            rhs_scale=h_planes[b][:, gauges],
                             start=(b == 0),
-                            stop=(b == R_PASSES - 1),
+                            stop=(b == R_BLOCKS - 1),
                         )
                 rows = slice(tiles.start, tiles.stop)
-                nc.vector.tensor_tensor(gap[:, rows, :], observed[:, rows, cols], bank[:], ALU.subtract)
+                nc.vector.tensor_tensor(gap[:, rows, :], observed[:, rows, gauges], bank[:], ALU.subtract)
             bounded = ring.tile([P, N_TILES, width], F32, name="bounded")
             nc.scalar.activation(bounded[:], gap[:], ACT.Tanh)
-            nc.sync.dma_start(out.rearrange("(u p) j -> p u j", p=P)[:, :, cols], bounded[:])
+            nc.sync.dma_start(out.rearrange("(u p) j -> p u j", p=P)[:, :, gauges], bounded[:])
 
         gather(0, 0)
         gather(1, 0)
         gather(1, 1)
         gather(0, 1)
-        order_wc_scales(1)
-        banks = [(b, h, t) for b in range(R_PASSES) for h in range(HALVES) for t in range(PACK)]
-        steps = [(b, s) for b in range(R_PASSES) for s in range(STEPS)]
+        order_wc_planes(1)
+
+        banks = [(b, half, t) for b in range(R_BLOCKS) for half in range(HALVES) for t in range(PACK)]
+        steps = [(b, s) for b in range(R_BLOCKS) for s in range(STEPS)]
 
         def current_and_speed(n):
             if n < len(banks):
@@ -275,34 +283,34 @@ def tile_list_surge_gauge_monitor_kernel(
             if PACK <= n < len(steps) + PACK:
                 speed(*steps[n - PACK])
 
+        round_shape = [P, K_PASSES, PACK, P, PACK]
         for n in range(STEPS):
             current_and_speed(n)
-        wf_round[0] = keep.tile([P, K_PASSES, PACK, P, PACK], BF16, name="wf_round0", align_bytes=64)
+        wf_round[0] = keep.tile(round_shape, BF16, name="wf_round0", align_bytes=64)
         round_wf(0, 0, nc.vector.tensor_copy)
         order_wc_codes(1)
         round_wf(0, 1, nc.vector.tensor_copy)
         quantise_wf(0, "wf_codes0")
+
         for s in range(STEPS):
             current_and_speed(STEPS + s)
             drag(0, s)
-            if s == 1:
-                wf_round[1] = keep.tile(
-                    [P, K_PASSES, PACK, P, PACK], BF16, name="wf_round1", tag="speed0_1", align_bytes=64
-                )
+            if s == ROUND_AFTER:
+                wf_round[1] = keep.tile(round_shape, BF16, name="wf_round1", tag="speed0_%d" % s, align_bytes=64)
                 round_wf(1, 0, nc.vector.tensor_copy)
                 round_wf(1, 1, nc.scalar.copy)
-            if s == 4:
-                quantise_wf(1, "speed0_4")
-            if s == 5:
-                quantise_drag(0, 0, 4)
-        spans = [(0, 2), (2, 4), (4, 6), (6, 7), (7, 8)]
+            if s == QUANTISE_WF_AFTER:
+                quantise_wf(1, "speed0_%d" % s)
+            if s == QUANTISE_H_AFTER:
+                quantise_drag(0, 0, STEPS // 2)
+
         for s in range(STEPS + 2):
             current_and_speed(2 * STEPS + s)
             if s < STEPS:
                 drag(1, s)
             if s == 0:
-                quantise_drag(0, 4, 8)
-            for lo, hi in spans:
+                quantise_drag(0, STEPS // 2, STEPS)
+            for lo, hi in SPANS:
                 if hi == s:
                     quantise_drag(1, lo, hi)
                 if hi + 1 == s:

@@ -28,10 +28,12 @@ HALF = 512
 HALVES = S // HALF
 STEP = 128
 STEPS = S // STEP
-RUN = 4
+PAIR = 2
 N_TILES = N // P
 SPANS = [(0, 2), (2, 4), (4, 6), (6, 7), (7, 8)]
-ROUND_AFTER, QUANTISE_WF_AFTER, QUANTISE_H_AFTER = 1, 4, 5
+QUANTISE_OWN_AFTER, ROUND_AFTER, QUANTISE_WF_AFTER, QUANTISE_H_AFTER = 0, 3, 5, 6
+SCALAR_SHARE = 64
+LEAD = 10
 
 
 def tile_list_surge_gauge_monitor_kernel(
@@ -40,9 +42,8 @@ def tile_list_surge_gauge_monitor_kernel(
     nc = tc.nc
     with ExitStack() as ctx:
         keep = ctx.enter_context(tc.tile_pool(name="keep", bufs=1))
-        late = ctx.enter_context(tc.tile_pool(name="late", bufs=1))
         mid = ctx.enter_context(tc.tile_pool(name="mid", bufs=1))
-        ring = ctx.enter_context(tc.tile_pool(name="ring", bufs=len(SPANS)))
+        late = ctx.enter_context(tc.tile_pool(name="late", bufs=1))
         psum_current = ctx.enter_context(tc.psum_pool(name="psum_current", bufs=3))
         psum_flow = ctx.enter_context(tc.psum_pool(name="psum_flow", bufs=3))
         psum_level = ctx.enter_context(tc.psum_pool(name="psum_level", bufs=2))
@@ -53,18 +54,18 @@ def tile_list_surge_gauge_monitor_kernel(
         one = keep.tile([P, 8], F32, name="one")
         background = keep.tile([P, 8], F32, name="background")
         wl_words_end = R_BLOCKS * N
-        packed_words = wl_words_end + R_BLOCKS * N // 4
+        packed_words = wl_words_end + PASS
         tab_rows = late.tile([P, T], U8, name="tab_rows", offset=4 * packed_words - T // 2)
         wc_rows = keep.tile([P, K_PASSES, H], U8, name="wc_rows")
         v_planes = [keep.tile([P, S], U8, name="v_plane%d" % g, align_bytes=64) for g in range(K_PASSES)]
-        nc.gpsimd.memset(tab_rows[:].bitcast(I32), 0)
-        nc.vector.memset(wc_rows[:].bitcast(I32), 0)
+        nc.vector.memset(tab_rows[:].bitcast(I32), 0)
+        nc.gpsimd.memset(wc_rows[:].bitcast(I32), 0)
         nc.vector.memset(one[:], 1.0)
         nc.scalar.activation(background[:], one[:], ACT.Sqrt)
         nc.vector.memset(v_planes[1][:].bitcast(I32), 0)
 
         wc_hbm = wc_words.rearrange("g p c -> p g c").bitcast(I32)
-        wc_raw = [keep.tile([P, PASS], I32, name="wc_raw%d" % b)[:] for b in range(R_BLOCKS)]
+        wc_raw = {0: keep.tile([P, PASS], I32, name="wc_raw0")[:]}
         table = [keep.tile([P, T], I32, name="table%d" % g) for g in range(K_PASSES)]
         wf_raw = {}
 
@@ -92,12 +93,12 @@ def tile_list_surge_gauge_monitor_kernel(
 
         load_wc(0)
         for e in range(2):
-            nc.sync.dma_start(tab_rows[e:P:GROUP, :].bitcast(I32), tab_scales[0, e::2, :].bitcast(I32))
-        nc.sync.dma_start(tab_rows[2:P:8, :].bitcast(I32), tab_scales[1].bitcast(I32))
+            nc.sync.dma_start(
+                tab_rows[e:P:8, :].bitcast(I32), tab_scales[:, e::2, :].rearrange("g y c -> y g c").bitcast(I32)
+            )
         load_table(0)
         load_planes(wc_rows, wc_scales)
         load_table(1)
-        load_wc(1)
 
         wc_codes = {0: keep.tile([P, K_PASSES, 2 * PASS], U8, name="wc_codes0", align_bytes=64)[:]}
         wc_planes = {0: keep.tile([P, K_PASSES, PASS], U8, name="wc_planes0", align_bytes=64)[:]}
@@ -120,7 +121,7 @@ def tile_list_surge_gauge_monitor_kernel(
         picked = picked_rows[:].bitcast(I32)
         nc.vector.tensor_copy(v_planes[0][:].bitcast(I32), picked)
         for e in range(PLANE_ROWS):
-            nc.sync.dma_start(v_planes[1][e:P:QUADRANT, :].bitcast(I32), picked[8 * e + 2 : P : QUADRANT, :])
+            nc.sync.dma_start(v_planes[1][e:P:QUADRANT, :].bitcast(I32), picked[GROUP * (e // 2) + 8 + e % 2 : P : QUADRANT, :])
         for e in range(2):
             nc.sync.dma_start(v_planes[0][2 + e : P : QUADRANT, :].bitcast(I32), picked[GROUP + e : P : QUADRANT, :])
         order_wc_planes(0)
@@ -129,6 +130,8 @@ def tile_list_surge_gauge_monitor_kernel(
         pieces = R_BLOCKS * K_PASSES
         packed = late.tile([P, packed_words], I32, name="packed", offset=0, align_bytes=64)
         floats = late.tile([P, pieces * piece + N_TILES * S], F32, name="floats", offset=4 * packed_words)
+        wc_raw[1] = packed[:, wl_words_end:]
+        load_wc(1)
         for b in range(R_BLOCKS):
             for g in range(K_PASSES):
                 first = (b * K_PASSES + g) * piece
@@ -136,15 +139,9 @@ def tile_list_surge_gauge_monitor_kernel(
                 load_wf(b, g)
         wl_codes = packed[:, :wl_words_end].rearrange("p (b c) -> p b c", b=R_BLOCKS)
         nc.sync.dma_start(wl_codes, wl_words.rearrange("b p c i -> p b (c i)").bitcast(I32))
-        nc.gpsimd.memset(packed[:, wl_words_end:], 0)
-        wl_planes = packed[:, wl_words_end:].bitcast(U8).rearrange("p (b c) -> p b c", b=R_BLOCKS)
-        load_planes(wl_planes, wl_scales)
         observed = floats[:, pieces * piece :].rearrange("p (u j) -> p u j", u=N_TILES)
         nc.sync.dma_start(observed, obs.rearrange("(u p) j -> p u j", p=P))
 
-        wc_second = mid.tile([P, 3 * K_PASSES * PASS], U8, name="wc_second", offset=4 * HALF, align_bytes=64)
-        wc_codes[1] = wc_second[:, : 2 * K_PASSES * PASS].rearrange("p (g c) -> p g c", g=K_PASSES)
-        wc_planes[1] = wc_second[:, 2 * K_PASSES * PASS :].rearrange("p (g c) -> p g c", g=K_PASSES)
         v_codes = {
             (0, 0): keep.tile([P, HALF], U32, name="v_codes00", align_bytes=64),
             (1, 0): keep.tile([P, HALF], U32, name="v_codes10", align_bytes=64),
@@ -157,7 +154,7 @@ def tile_list_surge_gauge_monitor_kernel(
             nc.vector.tensor_copy(v_codes[g, half][:], table[g][:].bitcast(U32).indirect(entries))
 
         squares = {
-            (b, half): keep.tile([P, HALF // RUN, PACK, RUN], F32, name="square%d_%d" % (b, half))
+            (b, half): keep.tile([P, HALF // 4, PACK, 2, PAIR], F32, name="square%d_%d" % (b, half))
             for b in range(R_BLOCKS)
             for half in range(HALVES)
         }
@@ -176,38 +173,39 @@ def tile_list_surge_gauge_monitor_kernel(
                     stop=(g == K_PASSES - 1),
                 )
             nc.scalar.activation(
-                squares[b, half][:, :, t, :], bank[:].rearrange("p (c i) -> p c i", i=RUN), ACT.Square
+                squares[b, half][:, :, t], bank[:].rearrange("p (h c i) -> p c h i", h=2, i=PAIR), ACT.Square
             )
 
         def speed(b, s):
             half, first = divmod(s * STEP, HALF)
-            root = keep.tile([P, STEP // RUN, PACK, RUN], F32, name="speed%d_%d" % (b, s), align_bytes=64)
-            nc.scalar.activation(
-                root[:], squares[b, half][:, first // RUN : (first + STEP) // RUN], ACT.Sqrt, bias=background[:, :1]
-            )
+            side, first = divmod(first, HALF // 2)
+            pairs = slice(first // PAIR, (first + STEP) // PAIR)
+            root = keep.tile([P, STEP // PAIR, PACK, PAIR], F32, name="speed%d_%d" % (b, s), align_bytes=64)
+            nc.scalar.activation(root[:], squares[b, half][:, pairs, :, side], ACT.Sqrt, bias=background[:, :1])
             speeds[b, s] = root
 
         wf_codes = {}
         wf_planes = {}
         wf_round = {}
 
-        def round_wf(b, g, copy):
+        def round_wf(b, g, copy, lo=0, hi=P):
+            if (b, g) not in wf_round:
+                wf_round[b, g] = keep.tile([P, PACK, P, PACK], BF16, name="wf_round%d_%d" % (b, g), align_bytes=64)
             copy(
-                wf_round[b][:, g].rearrange("p t m i -> p m i t"),
-                wf_raw[b, g].rearrange("p (i m t) -> p m i t", i=PACK, t=PACK),
+                wf_round[b, g][:].rearrange("p t m i -> p m i t")[:, lo:hi],
+                wf_raw[b, g].rearrange("p (i m t) -> p m i t", i=PACK, t=PACK)[:, lo:hi],
             )
 
-        def quantise_wf(b, tag):
-            codes = keep.tile([P, K_PASSES * PASS], U32, name="wf_codes%d" % b, tag=tag, align_bytes=64)
-            planes = keep.tile([P, K_PASSES * PASS], U8, name="wf_planes%d" % b, align_bytes=64)
+        def quantise_wf(b, g):
+            codes = keep.tile([P, PASS], U32, name="wf_codes%d_%d" % (b, g), align_bytes=64)
+            planes = keep.tile([P, PASS], U8, name="wf_planes%d_%d" % (b, g), align_bytes=64)
             nc.vector.quantize_mx(
                 out=codes[:].bitcast(FP8X4),
                 scales=planes[:],
-                in_=wf_round[b][:].rearrange("p g t m i -> p (g t m i)"),
+                in_=wf_round[b, g][:].rearrange("p t m i -> p (t m i)"),
             )
-            for g in range(K_PASSES):
-                wf_codes[b, g] = codes[:, g * PASS : (g + 1) * PASS]
-                wf_planes[b, g] = planes[:, g * PASS : (g + 1) * PASS]
+            wf_codes[b, g] = codes
+            wf_planes[b, g] = planes
 
         drags = [keep.tile([P, S, PACK], BF16, name="drag%d" % b, align_bytes=64) for b in range(R_BLOCKS)]
         h_codes = [keep.tile([P, S], U32, name="h_codes%d" % b, align_bytes=64) for b in range(R_BLOCKS)]
@@ -229,8 +227,8 @@ def tile_list_surge_gauge_monitor_kernel(
                         stop=(g == K_PASSES - 1),
                     )
             nc.vector.tensor_tensor(
-                drags[b][:, gauges, :].rearrange("p (c i) t -> p c t i", i=RUN),
-                bank[:].rearrange("p t (c i) -> p c t i", i=RUN),
+                drags[b][:, gauges, :].rearrange("p (c i) t -> p c t i", i=PAIR),
+                bank[:].rearrange("p t (c i) -> p c t i", i=PAIR),
                 speeds[b, s][:],
                 ALU.mult,
             )
@@ -247,7 +245,7 @@ def tile_list_surge_gauge_monitor_kernel(
             gauges = slice(lo * STEP, hi * STEP)
             width = (hi - lo) * STEP
             per_bank = min(N_TILES, HALF // width)
-            gap = ring.tile([P, N_TILES, width], F32, name="gap")
+            gap = keep.tile([P, N_TILES, width], F32, name="gap%d" % lo)
             for first in range(0, N_TILES, per_bank):
                 tiles = range(first, min(first + per_bank, N_TILES))
                 bank = psum_level.tile([P, len(tiles), width], F32, name="level_bank")
@@ -264,49 +262,55 @@ def tile_list_surge_gauge_monitor_kernel(
                         )
                 rows = slice(tiles.start, tiles.stop)
                 nc.vector.tensor_tensor(gap[:, rows, :], observed[:, rows, gauges], bank[:], ALU.subtract)
-            bounded = ring.tile([P, N_TILES, width], F32, name="bounded")
-            nc.scalar.activation(bounded[:], gap[:], ACT.Tanh)
-            nc.sync.dma_start(out.rearrange("(u p) j -> p u j", p=P)[:, :, gauges], bounded[:])
+            result = bounded[:, N_TILES * lo * STEP : N_TILES * hi * STEP].rearrange("p (u j) -> p u j", u=N_TILES)
+            nc.scalar.activation(result, gap[:], ACT.Tanh)
+            nc.sync.dma_start(out.rearrange("(u p) j -> p u j", p=P)[:, :, gauges], result)
 
         gather(0, 0)
         gather(1, 0)
         gather(1, 1)
         gather(0, 1)
+
+        wc_second = mid.tile([P, 3 * K_PASSES * PASS], U8, name="wc_second", offset=4 * HALF, align_bytes=64)
+        wc_codes[1] = wc_second[:, : 2 * K_PASSES * PASS].rearrange("p (g c) -> p g c", g=K_PASSES)
+        wc_planes[1] = wc_second[:, 2 * K_PASSES * PASS :].rearrange("p (g c) -> p g c", g=K_PASSES)
+        order_wc_codes(1)
         order_wc_planes(1)
+        wl_planes = wc_rows[:, :, PASS : PASS + N]
 
         banks = [(b, half, t) for b in range(R_BLOCKS) for half in range(HALVES) for t in range(PACK)]
-        steps = [(b, s) for b in range(R_BLOCKS) for s in range(STEPS)]
+        for n in range(LEAD):
+            current(*banks[n])
+        for g in range(K_PASSES):
+            round_wf(0, g, nc.vector.tensor_copy)
+            quantise_wf(0, g)
+        load_planes(wl_planes, wl_scales)
+        round_wf(1, 0, nc.vector.tensor_copy)
 
-        def current_and_speed(n):
-            if n < len(banks):
+        def speed_and_current(b, s):
+            speed(b, s)
+            n = LEAD + (b * STEPS + s) // 2
+            if s % 2 == 1 and n < len(banks):
                 current(*banks[n])
-            if PACK <= n < len(steps) + PACK:
-                speed(*steps[n - PACK])
-
-        round_shape = [P, K_PASSES, PACK, P, PACK]
-        for n in range(STEPS):
-            current_and_speed(n)
-        wf_round[0] = keep.tile(round_shape, BF16, name="wf_round0", align_bytes=64)
-        round_wf(0, 0, nc.vector.tensor_copy)
-        order_wc_codes(1)
-        round_wf(0, 1, nc.vector.tensor_copy)
-        quantise_wf(0, "wf_codes0")
 
         for s in range(STEPS):
-            current_and_speed(STEPS + s)
+            speed_and_current(0, s)
             drag(0, s)
+            if s == QUANTISE_OWN_AFTER:
+                quantise_wf(1, 0)
             if s == ROUND_AFTER:
-                wf_round[1] = keep.tile(round_shape, BF16, name="wf_round1", tag="speed0_%d" % s, align_bytes=64)
-                round_wf(1, 0, nc.vector.tensor_copy)
-                round_wf(1, 1, nc.scalar.copy)
+                round_wf(1, 1, nc.scalar.copy, 0, SCALAR_SHARE)
+                round_wf(1, 1, nc.vector.tensor_copy, SCALAR_SHARE, P)
             if s == QUANTISE_WF_AFTER:
-                quantise_wf(1, "speed0_%d" % s)
+                quantise_wf(1, 1)
             if s == QUANTISE_H_AFTER:
                 quantise_drag(0, 0, STEPS // 2)
 
+        bounded = keep.tile([P, N_TILES * S], F32, name="bounded", tag="square1_1")
+
         for s in range(STEPS + 2):
-            current_and_speed(2 * STEPS + s)
             if s < STEPS:
+                speed_and_current(1, s)
                 drag(1, s)
             if s == 0:
                 quantise_drag(0, STEPS // 2, STEPS)

@@ -31,8 +31,7 @@ STEPS = S // STEP
 PAIR = 2
 N_TILES = N // P
 SPANS = [(0, 2), (2, 4), (4, 6), (6, 7), (7, 8)]
-QUANTISE_OWN_AFTER, ROUND_AFTER, QUANTISE_WF_AFTER, QUANTISE_H_AFTER = 0, 3, 5, 6
-SCALAR_SHARE = 64
+QUANTISE_OWN_AFTER, ROUND_AFTER, QUANTISE_WF_AFTER, QUANTISE_H_AFTER = 0, 3, 3, 4
 LEAD = 10
 
 
@@ -43,6 +42,7 @@ def tile_list_surge_gauge_monitor_kernel(
     with ExitStack() as ctx:
         keep = ctx.enter_context(tc.tile_pool(name="keep", bufs=1))
         mid = ctx.enter_context(tc.tile_pool(name="mid", bufs=1))
+        turns = ctx.enter_context(tc.tile_pool(name="turns", bufs=1))
         late = ctx.enter_context(tc.tile_pool(name="late", bufs=1))
         psum_current = ctx.enter_context(tc.psum_pool(name="psum_current", bufs=3))
         psum_flow = ctx.enter_context(tc.psum_pool(name="psum_flow", bufs=3))
@@ -53,9 +53,7 @@ def tile_list_surge_gauge_monitor_kernel(
 
         one = keep.tile([P, 8], F32, name="one")
         background = keep.tile([P, 8], F32, name="background")
-        wl_words_end = R_BLOCKS * N
-        packed_words = wl_words_end + PASS
-        tab_rows = late.tile([P, T], U8, name="tab_rows", offset=4 * packed_words - T // 2)
+        tab_rows = late.tile([P, T], U8, name="tab_rows", offset=4 * PASS - T // 2)
         wc_rows = keep.tile([P, K_PASSES, H], U8, name="wc_rows")
         v_planes = [keep.tile([P, S], U8, name="v_plane%d" % g, align_bytes=64) for g in range(K_PASSES)]
         nc.vector.memset(tab_rows[:].bitcast(I32), 0)
@@ -66,7 +64,7 @@ def tile_list_surge_gauge_monitor_kernel(
 
         wc_hbm = wc_words.rearrange("g p c -> p g c").bitcast(I32)
         wc_raw = {0: keep.tile([P, PASS], I32, name="wc_raw0")[:]}
-        table = [keep.tile([P, T], I32, name="table%d" % g) for g in range(K_PASSES)]
+        table = [turns.tile([P, T], I32, name="table0", offset=0), keep.tile([P, T], I32, name="table1", align_bytes=64)]
         wf_raw = {}
 
         def load_wc(b):
@@ -127,20 +125,13 @@ def tile_list_surge_gauge_monitor_kernel(
         order_wc_planes(0)
 
         piece = PACK * PASS
-        pieces = R_BLOCKS * K_PASSES
-        packed = late.tile([P, packed_words], I32, name="packed", offset=0, align_bytes=64)
-        floats = late.tile([P, pieces * piece + N_TILES * S], F32, name="floats", offset=4 * packed_words)
-        wc_raw[1] = packed[:, wl_words_end:]
-        load_wc(1)
-        for b in range(R_BLOCKS):
-            for g in range(K_PASSES):
-                first = (b * K_PASSES + g) * piece
-                wf_raw[b, g] = floats[:, first : first + piece]
-                load_wf(b, g)
-        wl_codes = packed[:, :wl_words_end].rearrange("p (b c) -> p b c", b=R_BLOCKS)
-        nc.sync.dma_start(wl_codes, wl_words.rearrange("b p c i -> p b (c i)").bitcast(I32))
-        observed = floats[:, pieces * piece :].rearrange("p (u j) -> p u j", u=N_TILES)
-        nc.sync.dma_start(observed, obs.rearrange("(u p) j -> p u j", p=P))
+        wc_raw[1] = late.tile([P, PASS], I32, name="wc_raw1", offset=0)[:]
+        wf_first = late.tile([P, K_PASSES * piece], F32, name="wf_first", offset=4 * PASS)
+        for g in range(K_PASSES):
+            wf_raw[0, g] = wf_first[:, g * piece : (g + 1) * piece]
+            load_wf(0, g)
+            if g == 0:
+                load_wc(1)
 
         v_codes = {
             (0, 0): keep.tile([P, HALF], U32, name="v_codes00", align_bytes=64),
@@ -153,10 +144,10 @@ def tile_list_surge_gauge_monitor_kernel(
             entries = lists[:, half * HALF // GROUP : (half + 1) * HALF // GROUP]
             nc.vector.tensor_copy(v_codes[g, half][:], table[g][:].bitcast(U32).indirect(entries))
 
+        square_shape = [P, HALF // 4, PACK, 2, PAIR]
         squares = {
-            (b, half): keep.tile([P, HALF // 4, PACK, 2, PAIR], F32, name="square%d_%d" % (b, half))
-            for b in range(R_BLOCKS)
-            for half in range(HALVES)
+            (b, half): keep.tile(square_shape, F32, name="square%d_%d" % (b, half))
+            for b, half in ((0, 0), (0, 1), (1, 0))
         }
         speeds = {}
 
@@ -180,7 +171,13 @@ def tile_list_surge_gauge_monitor_kernel(
             half, first = divmod(s * STEP, HALF)
             side, first = divmod(first, HALF // 2)
             pairs = slice(first // PAIR, (first + STEP) // PAIR)
-            root = keep.tile([P, STEP // PAIR, PACK, PAIR], F32, name="speed%d_%d" % (b, s), align_bytes=64)
+            root_shape = [P, STEP // PAIR, PACK, PAIR]
+            if (b, s) == (0, ROUND_AFTER + 1):
+                root = turns.tile(root_shape, F32, name="speed_behind_rounding", offset=0)
+            elif (b, s) == (0, STEPS - 1):
+                root = keep.tile(root_shape, F32, name="speed_behind_quantise", tag="wf_round1_1", align_bytes=64)
+            else:
+                root = keep.tile(root_shape, F32, name="speed%d_%d" % (b, s), align_bytes=64)
             nc.scalar.activation(root[:], squares[b, half][:, pairs, :, side], ACT.Sqrt, bias=background[:, :1])
             speeds[b, s] = root
 
@@ -207,7 +204,7 @@ def tile_list_surge_gauge_monitor_kernel(
             wf_codes[b, g] = codes
             wf_planes[b, g] = planes
 
-        drags = [keep.tile([P, S, PACK], BF16, name="drag%d" % b, align_bytes=64) for b in range(R_BLOCKS)]
+        drags = {}
         h_codes = [keep.tile([P, S], U32, name="h_codes%d" % b, align_bytes=64) for b in range(R_BLOCKS)]
         h_planes = [keep.tile([P, S], U8, name="h_plane%d" % b, align_bytes=64) for b in range(R_BLOCKS)]
 
@@ -271,6 +268,10 @@ def tile_list_surge_gauge_monitor_kernel(
         gather(1, 1)
         gather(0, 1)
 
+        wf_raw[1, 0] = keep.tile([P, piece], F32, name="wf_raw10", tag="table1", align_bytes=64)[:]
+        wf_raw[1, 1] = turns.tile([P, piece], F32, name="wf_raw11", offset=0)[:]
+        for g in range(K_PASSES):
+            load_wf(1, g)
         wc_second = mid.tile([P, 3 * K_PASSES * PASS], U8, name="wc_second", offset=4 * HALF, align_bytes=64)
         wc_codes[1] = wc_second[:, : 2 * K_PASSES * PASS].rearrange("p (g c) -> p g c", g=K_PASSES)
         wc_planes[1] = wc_second[:, 2 * K_PASSES * PASS :].rearrange("p (g c) -> p g c", g=K_PASSES)
@@ -284,8 +285,14 @@ def tile_list_surge_gauge_monitor_kernel(
         for g in range(K_PASSES):
             round_wf(0, g, nc.vector.tensor_copy)
             quantise_wf(0, g)
+        wl_codes = late.tile([P, R_BLOCKS, N], I32, name="wl_codes", offset=4 * PASS, align_bytes=64)
+        nc.sync.dma_start(wl_codes[:], wl_words.rearrange("b p c i -> p b (c i)").bitcast(I32))
         load_planes(wl_planes, wl_scales)
+        observed = late.tile([P, N_TILES, S], F32, name="observed", offset=4 * (PASS + piece // 2))
+        nc.sync.dma_start(observed[:], obs.rearrange("(u p) j -> p u j", p=P))
         round_wf(1, 0, nc.vector.tensor_copy)
+        drags[0] = keep.tile([P, S, PACK], BF16, name="drag0", tag="table1", align_bytes=64)
+        drags[1] = keep.tile([P, S, PACK], BF16, name="drag1", align_bytes=64)
 
         def speed_and_current(b, s):
             speed(b, s)
@@ -299,14 +306,14 @@ def tile_list_surge_gauge_monitor_kernel(
             if s == QUANTISE_OWN_AFTER:
                 quantise_wf(1, 0)
             if s == ROUND_AFTER:
-                round_wf(1, 1, nc.scalar.copy, 0, SCALAR_SHARE)
-                round_wf(1, 1, nc.vector.tensor_copy, SCALAR_SHARE, P)
+                round_wf(1, 1, nc.scalar.copy)
+                squares[1, 1] = turns.tile(square_shape, F32, name="square1_1", offset=2 * piece)
             if s == QUANTISE_WF_AFTER:
                 quantise_wf(1, 1)
             if s == QUANTISE_H_AFTER:
                 quantise_drag(0, 0, STEPS // 2)
 
-        bounded = keep.tile([P, N_TILES * S], F32, name="bounded", tag="square1_1")
+        bounded = turns.tile([P, N_TILES * S], F32, name="bounded", offset=2 * piece)
 
         for s in range(STEPS + 2):
             if s < STEPS:

@@ -31,7 +31,10 @@ STEPS = S // STEP
 PAIR = 2
 N_TILES = N // P
 SPANS = [(0, 2), (2, 4), (4, 6), (6, 7), (7, 8)]
-QUANTISE_OWN_AFTER, ROUND_AFTER, QUANTISE_WF_AFTER, QUANTISE_H_AFTER = 0, 3, 3, 4
+PIECE = 4 * PACK * PASS
+WF_FIRST = PIECE + 3 * 512
+EDGE = 512
+SCALAR_SHARE = 64
 LEAD = 10
 
 
@@ -44,16 +47,14 @@ def tile_list_surge_gauge_monitor_kernel(
         mid = ctx.enter_context(tc.tile_pool(name="mid", bufs=1))
         turns = ctx.enter_context(tc.tile_pool(name="turns", bufs=1))
         late = ctx.enter_context(tc.tile_pool(name="late", bufs=1))
-        psum_current = ctx.enter_context(tc.psum_pool(name="psum_current", bufs=3))
-        psum_flow = ctx.enter_context(tc.psum_pool(name="psum_flow", bufs=3))
-        psum_level = ctx.enter_context(tc.psum_pool(name="psum_level", bufs=2))
+        psum = ctx.enter_context(tc.psum_pool(name="psum", bufs=8))
 
         lists = keep.tile([P, S // GROUP], U16, name="lists")
         nc.sync.dma_start(lists[:], offs)
 
         one = keep.tile([P, 8], F32, name="one")
         background = keep.tile([P, 8], F32, name="background")
-        tab_rows = late.tile([P, T], U8, name="tab_rows", offset=4 * PASS - T // 2)
+        tab_rows = late.tile([P, T], U8, name="tab_rows", offset=WF_FIRST - T // 2)
         wc_rows = keep.tile([P, K_PASSES, H], U8, name="wc_rows")
         v_planes = [keep.tile([P, S], U8, name="v_plane%d" % g, align_bytes=64) for g in range(K_PASSES)]
         nc.vector.memset(tab_rows[:].bitcast(I32), 0)
@@ -64,7 +65,7 @@ def tile_list_surge_gauge_monitor_kernel(
 
         wc_hbm = wc_words.rearrange("g p c -> p g c").bitcast(I32)
         wc_raw = {0: keep.tile([P, PASS], I32, name="wc_raw0")[:]}
-        table = [turns.tile([P, T], I32, name="table0", offset=0), keep.tile([P, T], I32, name="table1", align_bytes=64)]
+        table = [turns.tile([P, T], I32, name="table0", offset=0, align_bytes=64), keep.tile([P, T], I32, name="table1")]
         wf_raw = {}
 
         def load_wc(b):
@@ -114,9 +115,9 @@ def tile_list_surge_gauge_monitor_kernel(
             )
 
         order_wc_codes(0)
-        picked_rows = mid.tile([P, S], U8, name="picked_rows", offset=4 * HALF - S // 2, align_bytes=64)
-        nc.vector.tensor_copy(picked_rows[:], tab_rows[:].indirect(lists[:]))
-        picked = picked_rows[:].bitcast(I32)
+        picked_rows = mid.tile([P, S + 128], U8, name="picked_rows", offset=4 * HALF - 64, align_bytes=64)
+        nc.vector.tensor_copy(picked_rows[:, :S], tab_rows[:].indirect(lists[:]))
+        picked = picked_rows[:, :S].bitcast(I32)
         nc.vector.tensor_copy(v_planes[0][:].bitcast(I32), picked)
         for e in range(PLANE_ROWS):
             nc.sync.dma_start(v_planes[1][e:P:QUADRANT, :].bitcast(I32), picked[GROUP * (e // 2) + 8 + e % 2 : P : QUADRANT, :])
@@ -125,13 +126,12 @@ def tile_list_surge_gauge_monitor_kernel(
         order_wc_planes(0)
 
         piece = PACK * PASS
-        wc_raw[1] = late.tile([P, PASS], I32, name="wc_raw1", offset=0)[:]
-        wf_first = late.tile([P, K_PASSES * piece], F32, name="wf_first", offset=4 * PASS)
-        for g in range(K_PASSES):
-            wf_raw[0, g] = wf_first[:, g * piece : (g + 1) * piece]
-            load_wf(0, g)
-            if g == 0:
-                load_wc(1)
+        wc_raw[1] = late.tile([P, PASS], I32, name="wc_raw1", offset=WF_FIRST - 4 * PASS)[:]
+        wf_raw[0, 0] = late.tile([P, piece], F32, name="wf_raw00", offset=WF_FIRST)[:]
+        wf_raw[0, 1] = mid.tile([P, piece], F32, name="wf_raw01", offset=4 * HALF + S)[:]
+        load_wf(0, 0)
+        load_wc(1)
+        load_wf(0, 1)
 
         v_codes = {
             (0, 0): keep.tile([P, HALF], U32, name="v_codes00", align_bytes=64),
@@ -147,12 +147,12 @@ def tile_list_surge_gauge_monitor_kernel(
         square_shape = [P, HALF // 4, PACK, 2, PAIR]
         squares = {
             (b, half): keep.tile(square_shape, F32, name="square%d_%d" % (b, half))
-            for b, half in ((0, 0), (0, 1), (1, 0))
+            for b, half in ((0, 0),)
         }
         speeds = {}
 
         def current(b, half, t):
-            bank = psum_current.tile([P, HALF], F32, name="current_bank")
+            bank = psum.tile([P, HALF], F32, name="current", tag="bank")
             for g in range(K_PASSES):
                 nc.tensor.matmul_mx(
                     out=bank[:],
@@ -171,15 +171,11 @@ def tile_list_surge_gauge_monitor_kernel(
             half, first = divmod(s * STEP, HALF)
             side, first = divmod(first, HALF // 2)
             pairs = slice(first // PAIR, (first + STEP) // PAIR)
-            root_shape = [P, STEP // PAIR, PACK, PAIR]
-            if (b, s) == (0, ROUND_AFTER + 1):
-                root = turns.tile(root_shape, F32, name="speed_behind_rounding", offset=0)
-            elif (b, s) == (0, STEPS - 1):
-                root = keep.tile(root_shape, F32, name="speed_behind_quantise", tag="wf_round1_1", align_bytes=64)
+            if (b, s) == (0, STEPS - 1):
+                speeds[b, s] = keep.tile([P, STEP // PAIR, PACK, PAIR], F32, name="last_speed", align_bytes=64)[:]
             else:
-                root = keep.tile(root_shape, F32, name="speed%d_%d" % (b, s), align_bytes=64)
-            nc.scalar.activation(root[:], squares[b, half][:, pairs, :, side], ACT.Sqrt, bias=background[:, :1])
-            speeds[b, s] = root
+                speeds[b, s] = speeds[b][:, s]
+            nc.scalar.activation(speeds[b, s], squares[b, half][:, pairs, :, side], ACT.Sqrt, bias=background[:, :1])
 
         wf_codes = {}
         wf_planes = {}
@@ -194,7 +190,12 @@ def tile_list_surge_gauge_monitor_kernel(
             )
 
         def quantise_wf(b, g):
-            codes = keep.tile([P, PASS], U32, name="wf_codes%d_%d" % (b, g), align_bytes=64)
+            if b + g == 0:
+                codes = mid.tile([P, PASS], U32, name="wf_codes0_0", offset=4 * HALF + S, align_bytes=64)
+            elif b + g == 2:
+                codes = keep.tile([P, PASS], U32, name="wf_codes1_1", tag="last_speed", align_bytes=64)
+            else:
+                codes = keep.tile([P, PASS], U32, name="wf_codes%d_%d" % (b, g), align_bytes=64)
             planes = keep.tile([P, PASS], U8, name="wf_planes%d_%d" % (b, g), align_bytes=64)
             nc.vector.quantize_mx(
                 out=codes[:].bitcast(FP8X4),
@@ -211,7 +212,7 @@ def tile_list_surge_gauge_monitor_kernel(
         def drag(b, s):
             gauges = slice(s * STEP, (s + 1) * STEP)
             half, first = divmod(s * STEP, HALF)
-            bank = psum_flow.tile([P, PACK, STEP], F32, name="flow_bank")
+            bank = psum.tile([P, PACK, STEP], F32, name="flow", tag="bank")
             for t in range(PACK):
                 for g in range(K_PASSES):
                     nc.tensor.matmul_mx(
@@ -226,7 +227,7 @@ def tile_list_surge_gauge_monitor_kernel(
             nc.vector.tensor_tensor(
                 drags[b][:, gauges, :].rearrange("p (c i) t -> p c t i", i=PAIR),
                 bank[:].rearrange("p t (c i) -> p c t i", i=PAIR),
-                speeds[b, s][:],
+                speeds[b, s],
                 ALU.mult,
             )
 
@@ -245,7 +246,7 @@ def tile_list_surge_gauge_monitor_kernel(
             gap = keep.tile([P, N_TILES, width], F32, name="gap%d" % lo)
             for first in range(0, N_TILES, per_bank):
                 tiles = range(first, min(first + per_bank, N_TILES))
-                bank = psum_level.tile([P, len(tiles), width], F32, name="level_bank")
+                bank = psum.tile([P, len(tiles), width], F32, name="level", tag="bank")
                 for u in tiles:
                     for b in range(R_BLOCKS):
                         nc.tensor.matmul_mx(
@@ -268,59 +269,65 @@ def tile_list_surge_gauge_monitor_kernel(
         gather(1, 1)
         gather(0, 1)
 
-        wf_raw[1, 0] = keep.tile([P, piece], F32, name="wf_raw10", tag="table1", align_bytes=64)[:]
-        wf_raw[1, 1] = turns.tile([P, piece], F32, name="wf_raw11", offset=0)[:]
-        for g in range(K_PASSES):
-            load_wf(1, g)
-        wc_second = mid.tile([P, 3 * K_PASSES * PASS], U8, name="wc_second", offset=4 * HALF, align_bytes=64)
-        wc_codes[1] = wc_second[:, : 2 * K_PASSES * PASS].rearrange("p (g c) -> p g c", g=K_PASSES)
-        wc_planes[1] = wc_second[:, 2 * K_PASSES * PASS :].rearrange("p (g c) -> p g c", g=K_PASSES)
+        wf_raw[1, 0] = turns.tile([P, piece], F32, name="wf_raw10", offset=0, align_bytes=64)[:]
+        load_wf(1, 0)
+        wc_codes[1] = keep.tile([P, K_PASSES, 2 * PASS], U8, name="wc_codes1", align_bytes=64)[:]
+        wc_planes[1] = mid.tile([P, K_PASSES, PASS], U8, name="wc_planes1", offset=4 * HALF, align_bytes=64)[:]
         order_wc_codes(1)
+        wf_raw[1, 1] = late.tile([P, piece], F32, name="wf_raw11", offset=0)[:]
+        load_wf(1, 1)
         order_wc_planes(1)
         wl_planes = wc_rows[:, :, PASS : PASS + N]
 
         banks = [(b, half, t) for b in range(R_BLOCKS) for half in range(HALVES) for t in range(PACK)]
-        for n in range(LEAD):
-            current(*banks[n])
-        for g in range(K_PASSES):
-            round_wf(0, g, nc.vector.tensor_copy)
-            quantise_wf(0, g)
-        wl_codes = late.tile([P, R_BLOCKS, N], I32, name="wl_codes", offset=4 * PASS, align_bytes=64)
+        for bank in banks[:PACK]:
+            current(*bank)
+        round_wf(0, 0, nc.scalar.copy, 0, SCALAR_SHARE)
+        round_wf(0, 0, nc.vector.tensor_copy, SCALAR_SHARE, P)
+        round_wf(0, 1, nc.vector.tensor_copy)
+        quantise_wf(0, 0)
+        quantise_wf(0, 1)
+        later = late.tile([P, 5 * piece], F32, name="later", offset=WF_FIRST + PIECE - EDGE)
+        for n, key in enumerate(((0, 1), (1, 0), (1, 1))):
+            squares[key] = later[:, n * piece : (n + 1) * piece].rearrange("p (c t h i) -> p c t h i", t=PACK, h=2, i=PAIR)
+        speed_shape = [P, STEPS, STEP // PAIR, PACK, PAIR]
+        speeds[0] = later[:, 3 * piece :].rearrange("p (s c t i) -> p s c t i", s=STEPS, t=PACK, i=PAIR)
+        speeds[1] = keep.tile(speed_shape, F32, name="speeds1")
+        for bank in banks[PACK:LEAD]:
+            current(*bank)
+        wl_codes = late.tile([P, R_BLOCKS, N], I32, name="wl_codes", offset=WF_FIRST + EDGE, align_bytes=64)
         nc.sync.dma_start(wl_codes[:], wl_words.rearrange("b p c i -> p b (c i)").bitcast(I32))
         load_planes(wl_planes, wl_scales)
-        observed = late.tile([P, N_TILES, S], F32, name="observed", offset=4 * (PASS + piece // 2))
+        observed = mid.tile([P, N_TILES, S], F32, name="observed", offset=4 * HALF + S + 4 * PASS)
         nc.sync.dma_start(observed[:], obs.rearrange("(u p) j -> p u j", p=P))
         round_wf(1, 0, nc.vector.tensor_copy)
-        drags[0] = keep.tile([P, S, PACK], BF16, name="drag0", tag="table1", align_bytes=64)
+        drags[0] = turns.tile([P, S, PACK], BF16, name="drag0", offset=4 * PASS, align_bytes=64)
         drags[1] = keep.tile([P, S, PACK], BF16, name="drag1", align_bytes=64)
 
         def speed_and_current(b, s):
             speed(b, s)
-            n = LEAD + (b * STEPS + s) // 2
-            if s % 2 == 1 and n < len(banks):
-                current(*banks[n])
+            if b == 0 and s % 2 == 1 and LEAD + s // 2 < len(banks) - PACK:
+                current(*banks[LEAD + s // 2])
+            if (b, s) == (1, PACK - 1):
+                for bank in banks[-PACK:]:
+                    current(*bank)
 
         for s in range(STEPS):
             speed_and_current(0, s)
             drag(0, s)
-            if s == QUANTISE_OWN_AFTER:
+            if s == 0:
                 quantise_wf(1, 0)
-            if s == ROUND_AFTER:
-                round_wf(1, 1, nc.scalar.copy)
-                squares[1, 1] = turns.tile(square_shape, F32, name="square1_1", offset=2 * piece)
-            if s == QUANTISE_WF_AFTER:
-                quantise_wf(1, 1)
-            if s == QUANTISE_H_AFTER:
-                quantise_drag(0, 0, STEPS // 2)
+                wf_round[1, 1] = keep.tile([P, PACK, P, PACK], BF16, name="wf_round1_1", tag="wf_round1_0", align_bytes=64)
+                nc.gpsimd.tensor_copy(wf_round[1, 1][:], wf_raw[1, 1].rearrange("p (i m t) -> p t m i", i=PACK, t=PACK))
+        quantise_wf(1, 1)
+        quantise_drag(0, 0, STEPS)
 
-        bounded = turns.tile([P, N_TILES * S], F32, name="bounded", offset=2 * piece)
+        bounded = late.tile([P, N_TILES * S], F32, name="bounded", offset=WF_FIRST + PIECE - EDGE)
 
         for s in range(STEPS + 2):
             if s < STEPS:
                 speed_and_current(1, s)
                 drag(1, s)
-            if s == 0:
-                quantise_drag(0, STEPS // 2, STEPS)
             for lo, hi in SPANS:
                 if hi == s:
                     quantise_drag(1, lo, hi)

@@ -35,7 +35,7 @@ PIECE = 4 * PACK * PASS
 WF_FIRST = PIECE + 3 * 512
 EDGE = 512
 SCALAR_SHARE = 64
-LEAD = 10
+LEAD = 8
 
 
 def tile_list_surge_gauge_monitor_kernel(

@@ -35,6 +35,7 @@ PIECE = 4 * PACK * PASS
 WF_FIRST = PIECE + 3 * 512
 EDGE = 512
 SCALAR_SHARE = 64
+WARM_UPS = 4
 LEAD = 8
 
 
@@ -55,7 +56,7 @@ def tile_list_surge_gauge_monitor_kernel(
         one = keep.tile([P, 8], F32, name="one")
         background = keep.tile([P, 8], F32, name="background")
         tab_rows = late.tile([P, T], U8, name="tab_rows", offset=WF_FIRST - T // 2)
-        wc_rows = keep.tile([P, K_PASSES, H], U8, name="wc_rows")
+        wc_rows = keep.tile([P, K_PASSES, H], U8, name="wc_rows", align_bytes=64)
         v_planes = [keep.tile([P, S], U8, name="v_plane%d" % g, align_bytes=64) for g in range(K_PASSES)]
         nc.vector.memset(tab_rows[:].bitcast(I32), 0)
         nc.gpsimd.memset(wc_rows[:].bitcast(I32), 0)
@@ -264,6 +265,17 @@ def tile_list_surge_gauge_monitor_kernel(
             nc.scalar.activation(result, gap[:], ACT.Tanh)
             nc.sync.dma_start(out.rearrange("(u p) j -> p u j", p=P)[:, :, gauges], result)
 
+        idle = psum.tile([P, HALF], F32, name="idle", tag="bank")
+        for n in range(WARM_UPS):
+            nc.tensor.matmul_mx(
+                out=idle[:],
+                lhsT=table[0][:, :P].bitcast(FP8X4),
+                lhsT_scale=wc_rows[:, 0, :P],
+                rhs=wc_codes[0][:, 0].bitcast(FP4X4),
+                rhs_scale=wc_rows[:, 0, :HALF],
+                start=True,
+                stop=True,
+            )
         gather(0, 0)
         gather(1, 0)
         gather(1, 1)

@@ -30,13 +30,12 @@ STEP = 128
 STEPS = S // STEP
 PAIR = 2
 N_TILES = N // P
+BANKS = 8
+BANK_BYTES = 2048
+KIB = 1024
 SPANS = [(0, 2), (2, 4), (4, 6), (6, 7), (7, 8)]
-PIECE = 4 * PACK * PASS
-WF_FIRST = PIECE + 3 * 512
-EDGE = 512
-SCALAR_SHARE = 64
-WARM_UPS = 4
-LEAD = 8
+PIECE = PACK * PASS
+EARLY = 2
 
 
 def tile_list_surge_gauge_monitor_kernel(
@@ -45,38 +44,64 @@ def tile_list_surge_gauge_monitor_kernel(
     nc = tc.nc
     with ExitStack() as ctx:
         keep = ctx.enter_context(tc.tile_pool(name="keep", bufs=1))
-        mid = ctx.enter_context(tc.tile_pool(name="mid", bufs=1))
         turns = ctx.enter_context(tc.tile_pool(name="turns", bufs=1))
-        late = ctx.enter_context(tc.tile_pool(name="late", bufs=1))
-        psum = ctx.enter_context(tc.psum_pool(name="psum", bufs=8))
+        psum = ctx.enter_context(tc.psum_pool(name="psum", bufs=1))
+
+        def turn(name, shape, dtype, offset):
+            return turns.tile(shape, dtype, name=name, offset=offset, align_bytes=64)
+
+        free_banks = list(range(BANKS))
+        made = []
+
+        def take_bank(shape):
+            number = free_banks.pop(0)
+            made.append(number)
+            return number, psum.tile(shape, F32, name="bank%d" % len(made), offset=number * BANK_BYTES)
+
+        AT_TABLE = (0, 8 * KIB)
+        AT_SQUARES = 16 * KIB
+        AT_WC1 = 23 * KIB
+        AT_TAB_ROWS = 24 * KIB
+        AT_WF00 = 25 * KIB
+        AT_CODES01 = 37 * KIB
+        AT_PICKED = AT_CODES01 + 3 * KIB // 2
+        AT_WF01 = AT_CODES01 + 2 * KIB
+        AT_WC0 = 47 * KIB
+        AT_LAST_SQUARES = 54 * KIB
+        AT_LAST_SPEED = 66 * KIB
+        AT_ROUND = {(1, 0): 50 * KIB, (1, 1): 50 * KIB}
 
         lists = keep.tile([P, S // GROUP], U16, name="lists")
         nc.sync.dma_start(lists[:], offs)
 
+        tab_rows = turn("tab_rows", [P, T], U8, AT_TAB_ROWS)
+        wc_rows = keep.tile([P, K_PASSES, H], U8, name="wc_rows", align_bytes=64)
+        v_planes = keep.tile([P, K_PASSES * S], U8, name="v_planes", align_bytes=64)
         one = keep.tile([P, 8], F32, name="one")
         background = keep.tile([P, 8], F32, name="background")
-        tab_rows = late.tile([P, T], U8, name="tab_rows", offset=WF_FIRST - T // 2)
-        wc_rows = keep.tile([P, K_PASSES, H], U8, name="wc_rows", align_bytes=64)
-        v_planes = [keep.tile([P, S], U8, name="v_plane%d" % g, align_bytes=64) for g in range(K_PASSES)]
-        nc.vector.memset(tab_rows[:].bitcast(I32), 0)
-        nc.gpsimd.memset(wc_rows[:].bitcast(I32), 0)
+        nc.gpsimd.memset(tab_rows[:].bitcast(I32), 0)
+        nc.vector.memset(wc_rows[:].bitcast(I32), 0)
         nc.vector.memset(one[:], 1.0)
+        nc.vector.memset(v_planes[:].bitcast(I32), 0)
         nc.scalar.activation(background[:], one[:], ACT.Sqrt)
-        nc.vector.memset(v_planes[1][:].bitcast(I32), 0)
 
+        table = [turn("table%d" % g, [P, T], I32, AT_TABLE[g]) for g in range(K_PASSES)]
         wc_hbm = wc_words.rearrange("g p c -> p g c").bitcast(I32)
-        wc_raw = {0: keep.tile([P, PASS], I32, name="wc_raw0")[:]}
-        table = [turns.tile([P, T], I32, name="table0", offset=0, align_bytes=64), keep.tile([P, T], I32, name="table1")]
-        wf_raw = {}
-
-        def load_wc(b):
-            nc.sync.dma_start(
-                wc_raw[b].rearrange("p (g c) -> p g c", g=K_PASSES),
-                wc_hbm[:, :, b * PASS // 2 : (b + 1) * PASS // 2],
-            )
+        wc_raw = [turn("wc_raw0", [P, PASS], I32, AT_WC0), turn("wc_raw1", [P, PASS], I32, AT_WC1)]
+        wc_codes = [keep.tile([P, K_PASSES, 2 * PASS], U8, name="wc_codes%d" % b, align_bytes=64) for b in range(R_BLOCKS)]
 
         def load_table(g):
             nc.sync.dma_start(table[g][:], tab_words[g].rearrange("p t i -> p (t i)").bitcast(I32))
+
+        def load_wc(b):
+            nc.sync.dma_start(
+                wc_raw[b][:].rearrange("p (g c) -> p g c", g=K_PASSES),
+                wc_hbm[:, :, b * PASS // 2 : (b + 1) * PASS // 2],
+            )
+            nc.scalar.copy(
+                wc_codes[b][:].bitcast(U16).rearrange("p g (t m) -> p g t m", t=PACK),
+                wc_raw[b][:].bitcast(U16).rearrange("p (g m t) -> p g t m", g=K_PASSES, t=PACK),
+            )
 
         def load_planes(planes, scales):
             for e in range(PLANE_ROWS):
@@ -85,119 +110,132 @@ def tile_list_surge_gauge_monitor_kernel(
                     scales[:, e::PLANE_ROWS, :].rearrange("g d c -> d g c").bitcast(I32),
                 )
 
-        def load_wf(b, g):
-            nc.sync.dma_start(
-                wf_raw[b, g].rearrange("p (i c) -> p i c", i=PACK),
-                wf[g * PASS : (g + 1) * PASS, b * PASS : (b + 1) * PASS].rearrange("(p i) c -> p i c", i=PACK),
-            )
-
-        load_wc(0)
-        for e in range(2):
-            nc.sync.dma_start(
-                tab_rows[e:P:8, :].bitcast(I32), tab_scales[:, e::2, :].rearrange("g y c -> y g c").bitcast(I32)
-            )
-        load_table(0)
-        load_planes(wc_rows, wc_scales)
-        load_table(1)
-
-        wc_codes = {0: keep.tile([P, K_PASSES, 2 * PASS], U8, name="wc_codes0", align_bytes=64)[:]}
-        wc_planes = {0: keep.tile([P, K_PASSES, PASS], U8, name="wc_planes0", align_bytes=64)[:]}
-
-        def order_wc_codes(b):
-            nc.vector.tensor_copy(
-                wc_codes[b].bitcast(U16).rearrange("p g (t m) -> p g t m", t=PACK),
-                wc_raw[b].bitcast(U16).rearrange("p (g m t) -> p g t m", g=K_PASSES, t=PACK),
-            )
+        wc_planes = [keep.tile([P, K_PASSES, PASS], U8, name="wc_planes%d" % b, align_bytes=64) for b in range(R_BLOCKS)]
 
         def order_wc_planes(b):
             nc.vector.tensor_copy(
-                wc_planes[b].rearrange("p g (t m) -> p g t m", t=PACK),
+                wc_planes[b][:].rearrange("p g (t m) -> p g t m", t=PACK),
                 wc_rows[:, :, b * PASS : (b + 1) * PASS].rearrange("p g (m t) -> p g t m", t=PACK),
             )
 
-        order_wc_codes(0)
-        picked_rows = mid.tile([P, S + 128], U8, name="picked_rows", offset=4 * HALF - 64, align_bytes=64)
-        nc.vector.tensor_copy(picked_rows[:, :S], tab_rows[:].indirect(lists[:]))
-        picked = picked_rows[:, :S].bitcast(I32)
-        nc.vector.tensor_copy(v_planes[0][:].bitcast(I32), picked)
-        for e in range(PLANE_ROWS):
-            nc.sync.dma_start(v_planes[1][e:P:QUADRANT, :].bitcast(I32), picked[GROUP * (e // 2) + 8 + e % 2 : P : QUADRANT, :])
-        for e in range(2):
-            nc.sync.dma_start(v_planes[0][2 + e : P : QUADRANT, :].bitcast(I32), picked[GROUP + e : P : QUADRANT, :])
+        load_wc(0)
+        nc.sync.dma_start(
+            tab_rows[0:P:4, :].bitcast(I32), tab_scales.rearrange("g q c -> q g c").bitcast(I32)
+        )
+        load_table(0)
+        load_planes(wc_rows, wc_scales)
+        load_table(1)
+        picked = turn("picked", [P, S], U8, AT_PICKED)
+        nc.vector.tensor_copy(picked[:], tab_rows[:].indirect(lists[:]))
+        for first in range(0, P, QUADRANT):
+            nc.sync.dma_start(
+                v_planes[first : first + PLANE_ROWS, :].bitcast(I32),
+                picked[first : first + QUADRANT : 4, :].bitcast(I32),
+            )
+        load_wc(1)
         order_wc_planes(0)
 
-        piece = PACK * PASS
-        wc_raw[1] = late.tile([P, PASS], I32, name="wc_raw1", offset=WF_FIRST - 4 * PASS)[:]
-        wf_raw[0, 0] = late.tile([P, piece], F32, name="wf_raw00", offset=WF_FIRST)[:]
-        wf_raw[0, 1] = mid.tile([P, piece], F32, name="wf_raw01", offset=4 * HALF + S)[:]
-        load_wf(0, 0)
-        load_wc(1)
-        load_wf(0, 1)
-
-        v_codes = {
-            (0, 0): keep.tile([P, HALF], U32, name="v_codes00", align_bytes=64),
-            (1, 0): keep.tile([P, HALF], U32, name="v_codes10", align_bytes=64),
-            (1, 1): keep.tile([P, HALF], U32, name="v_codes11", align_bytes=64),
-            (0, 1): mid.tile([P, HALF], U32, name="v_codes01", offset=0, align_bytes=64),
+        wf_raw = {
+            (0, 0): turn("wf_raw00", [P, PIECE], F32, AT_WF00),
+            (0, 1): turn("wf_raw01", [P, PIECE], F32, AT_WF01),
+            (1, 0): turn("wf_raw10", [P, PIECE], F32, AT_TABLE[0]),
+            (1, 1): turn("wf_raw11", [P, PIECE], F32, AT_TABLE[1]),
         }
 
+        def load_wf(b, g):
+            nc.sync.dma_start(
+                wf_raw[b, g][:].rearrange("p (i c) -> p i c", i=PACK),
+                wf[g * PASS : (g + 1) * PASS, b * PASS : (b + 1) * PASS].rearrange("(p i) c -> p i c", i=PACK),
+            )
+
+        v_codes = {}
+
         def gather(g, half):
+            if (g, half) == (0, 1):
+                v_codes[g, half] = turn("v_codes01", [P, HALF], U32, AT_CODES01)
+            else:
+                v_codes[g, half] = keep.tile([P, HALF], U32, name="v_codes%d%d" % (g, half), align_bytes=64)
             entries = lists[:, half * HALF // GROUP : (half + 1) * HALF // GROUP]
             nc.vector.tensor_copy(v_codes[g, half][:], table[g][:].bitcast(U32).indirect(entries))
 
+        load_wf(0, 0)
+        load_wf(0, 1)
+        gather(0, 0)
+        order_wc_planes(1)
+        gather(1, 0)
+        gather(1, 1)
+        gather(0, 1)
+        load_wf(1, 0)
+        load_wf(1, 1)
+
         square_shape = [P, HALF // 4, PACK, 2, PAIR]
         squares = {
-            (b, half): keep.tile(square_shape, F32, name="square%d_%d" % (b, half))
-            for b, half in ((0, 0),)
+            (0, 0): turn("squares00", square_shape, F32, AT_SQUARES),
+            (0, 1): keep.tile(square_shape, F32, name="squares01"),
+            (1, 0): keep.tile(square_shape, F32, name="squares10"),
+            (1, 1): turn("squares11", square_shape, F32, AT_LAST_SQUARES),
         }
-        speeds = {}
+        currents = {}
 
         def current(b, half, t):
-            bank = psum.tile([P, HALF], F32, name="current", tag="bank")
-            for g in range(K_PASSES):
+            currents[b, half, t] = take_bank([P, HALF])
+            bank = currents[b, half, t][1]
+            passes = (0, 1) if len(made) <= EARLY else (1, 0)
+            for g in passes:
                 nc.tensor.matmul_mx(
                     out=bank[:],
                     lhsT=wc_codes[b][:, g, 2 * P * t : 2 * P * (t + 1)].bitcast(FP4X4),
                     lhsT_scale=wc_planes[b][:, g, P * t : P * (t + 1)],
                     rhs=v_codes[g, half][:].bitcast(FP8X4),
-                    rhs_scale=v_planes[g][:, half * HALF : (half + 1) * HALF],
-                    start=(g == 0),
-                    stop=(g == K_PASSES - 1),
+                    rhs_scale=v_planes[:, g * S + half * HALF : g * S + (half + 1) * HALF],
+                    start=(g == passes[0]),
+                    stop=(g == passes[-1]),
                 )
+
+        def square(b, half, t):
+            number, bank = currents[b, half, t]
             nc.scalar.activation(
                 squares[b, half][:, :, t], bank[:].rearrange("p (h c i) -> p c h i", h=2, i=PAIR), ACT.Square
             )
+            free_banks.append(number)
+
+        speeds = {}
 
         def speed(b, s):
             half, first = divmod(s * STEP, HALF)
             side, first = divmod(first, HALF // 2)
             pairs = slice(first // PAIR, (first + STEP) // PAIR)
+            shape = [P, STEP // PAIR, PACK, PAIR]
             if (b, s) == (0, STEPS - 1):
-                speeds[b, s] = keep.tile([P, STEP // PAIR, PACK, PAIR], F32, name="last_speed", align_bytes=64)[:]
+                speeds[b, s] = turn("last_speed", shape, F32, AT_LAST_SPEED)
             else:
-                speeds[b, s] = speeds[b][:, s]
-            nc.scalar.activation(speeds[b, s], squares[b, half][:, pairs, :, side], ACT.Sqrt, bias=background[:, :1])
+                speeds[b, s] = keep.tile(shape, F32, name="speed%d_%d" % (b, s))
+            nc.scalar.activation(speeds[b, s][:], squares[b, half][:, pairs, :, side], ACT.Sqrt, bias=background[:, :1])
 
         wf_codes = {}
         wf_planes = {}
         wf_round = {}
 
-        def round_wf(b, g, copy, lo=0, hi=P):
-            if (b, g) not in wf_round:
-                wf_round[b, g] = keep.tile([P, PACK, P, PACK], BF16, name="wf_round%d_%d" % (b, g), align_bytes=64)
-            copy(
-                wf_round[b, g][:].rearrange("p t m i -> p m i t")[:, lo:hi],
-                wf_raw[b, g].rearrange("p (i m t) -> p m i t", i=PACK, t=PACK)[:, lo:hi],
-            )
+        def round_wf(b, g):
+            shape = [P, PACK, P, PACK]
+            if (b, g) in AT_ROUND:
+                wf_round[b, g] = turn("wf_round%d%d" % (b, g), shape, BF16, AT_ROUND[b, g])
+            else:
+                wf_round[b, g] = keep.tile(shape, BF16, name="wf_round%d%d" % (b, g), align_bytes=64)
+            if (b, g) == (1, 1):
+                nc.gpsimd.tensor_copy(wf_round[b, g][:], wf_raw[b, g][:].rearrange("p (i m t) -> p t m i", i=PACK, t=PACK))
+            else:
+                nc.vector.tensor_copy(
+                    wf_round[b, g][:].rearrange("p t m i -> p m i t"),
+                    wf_raw[b, g][:].rearrange("p (i m t) -> p m i t", i=PACK, t=PACK),
+                )
 
         def quantise_wf(b, g):
-            if b + g == 0:
-                codes = mid.tile([P, PASS], U32, name="wf_codes0_0", offset=4 * HALF + S, align_bytes=64)
-            elif b + g == 2:
-                codes = keep.tile([P, PASS], U32, name="wf_codes1_1", tag="last_speed", align_bytes=64)
+            if (b, g) == (1, 1):
+                codes = turn("wf_codes11", [P, PASS], U32, AT_LAST_SPEED)
             else:
-                codes = keep.tile([P, PASS], U32, name="wf_codes%d_%d" % (b, g), align_bytes=64)
-            planes = keep.tile([P, PASS], U8, name="wf_planes%d_%d" % (b, g), align_bytes=64)
+                codes = keep.tile([P, PASS], U32, name="wf_codes%d%d" % (b, g), align_bytes=64)
+            planes = keep.tile([P, PASS], U8, name="wf_planes%d%d" % (b, g), align_bytes=64)
             nc.vector.quantize_mx(
                 out=codes[:].bitcast(FP8X4),
                 scales=planes[:],
@@ -213,7 +251,7 @@ def tile_list_surge_gauge_monitor_kernel(
         def drag(b, s):
             gauges = slice(s * STEP, (s + 1) * STEP)
             half, first = divmod(s * STEP, HALF)
-            bank = psum.tile([P, PACK, STEP], F32, name="flow", tag="bank")
+            number, bank = take_bank([P, PACK, STEP])
             for t in range(PACK):
                 for g in range(K_PASSES):
                     nc.tensor.matmul_mx(
@@ -221,16 +259,17 @@ def tile_list_surge_gauge_monitor_kernel(
                         lhsT=wf_codes[b, g][:, P * t : P * (t + 1)].bitcast(FP8X4),
                         lhsT_scale=wf_planes[b, g][:, P * t : P * (t + 1)],
                         rhs=v_codes[g, half][:, first : first + STEP].bitcast(FP8X4),
-                        rhs_scale=v_planes[g][:, gauges],
+                        rhs_scale=v_planes[:, g * S + s * STEP : g * S + (s + 1) * STEP],
                         start=(g == 0),
                         stop=(g == K_PASSES - 1),
                     )
             nc.vector.tensor_tensor(
                 drags[b][:, gauges, :].rearrange("p (c i) t -> p c t i", i=PAIR),
                 bank[:].rearrange("p t (c i) -> p c t i", i=PAIR),
-                speeds[b, s],
+                speeds[b, s][:],
                 ALU.mult,
             )
+            free_banks.append(number)
 
         def quantise_drag(b, lo, hi):
             gauges = slice(lo * STEP, hi * STEP)
@@ -247,7 +286,7 @@ def tile_list_surge_gauge_monitor_kernel(
             gap = keep.tile([P, N_TILES, width], F32, name="gap%d" % lo)
             for first in range(0, N_TILES, per_bank):
                 tiles = range(first, min(first + per_bank, N_TILES))
-                bank = psum.tile([P, len(tiles), width], F32, name="level", tag="bank")
+                number, bank = take_bank([P, len(tiles), width])
                 for u in tiles:
                     for b in range(R_BLOCKS):
                         nc.tensor.matmul_mx(
@@ -261,85 +300,52 @@ def tile_list_surge_gauge_monitor_kernel(
                         )
                 rows = slice(tiles.start, tiles.stop)
                 nc.vector.tensor_tensor(gap[:, rows, :], observed[:, rows, gauges], bank[:], ALU.subtract)
+                free_banks.append(number)
             result = bounded[:, N_TILES * lo * STEP : N_TILES * hi * STEP].rearrange("p (u j) -> p u j", u=N_TILES)
             nc.scalar.activation(result, gap[:], ACT.Tanh)
             nc.sync.dma_start(out.rearrange("(u p) j -> p u j", p=P)[:, :, gauges], result)
 
-        idle = psum.tile([P, HALF], F32, name="idle", tag="bank")
-        for n in range(WARM_UPS):
-            nc.tensor.matmul_mx(
-                out=idle[:],
-                lhsT=table[0][:, :P].bitcast(FP8X4),
-                lhsT_scale=wc_rows[:, 0, :P],
-                rhs=wc_codes[0][:, 0].bitcast(FP4X4),
-                rhs_scale=wc_rows[:, 0, :HALF],
-                start=True,
-                stop=True,
-            )
-        gather(0, 0)
-        gather(1, 0)
-        gather(1, 1)
-        gather(0, 1)
-
-        wf_raw[1, 0] = turns.tile([P, piece], F32, name="wf_raw10", offset=0, align_bytes=64)[:]
-        load_wf(1, 0)
-        wc_codes[1] = keep.tile([P, K_PASSES, 2 * PASS], U8, name="wc_codes1", align_bytes=64)[:]
-        wc_planes[1] = mid.tile([P, K_PASSES, PASS], U8, name="wc_planes1", offset=4 * HALF, align_bytes=64)[:]
-        order_wc_codes(1)
-        wf_raw[1, 1] = late.tile([P, piece], F32, name="wf_raw11", offset=0)[:]
-        load_wf(1, 1)
-        order_wc_planes(1)
-        wl_planes = wc_rows[:, :, PASS : PASS + N]
-
-        banks = [(b, half, t) for b in range(R_BLOCKS) for half in range(HALVES) for t in range(PACK)]
-        for bank in banks[:PACK]:
-            current(*bank)
-        round_wf(0, 0, nc.scalar.copy, 0, SCALAR_SHARE)
-        round_wf(0, 0, nc.vector.tensor_copy, SCALAR_SHARE, P)
-        round_wf(0, 1, nc.vector.tensor_copy)
+        for b, half in ((0, 0), (0, 1), (1, 0)):
+            for t in range(PACK):
+                current(b, half, t)
+                square(b, half, t)
+        round_wf(0, 0)
+        round_wf(0, 1)
         quantise_wf(0, 0)
         quantise_wf(0, 1)
-        later = late.tile([P, 5 * piece], F32, name="later", offset=WF_FIRST + PIECE - EDGE)
-        for n, key in enumerate(((0, 1), (1, 0), (1, 1))):
-            squares[key] = later[:, n * piece : (n + 1) * piece].rearrange("p (c t h i) -> p c t h i", t=PACK, h=2, i=PAIR)
-        speed_shape = [P, STEPS, STEP // PAIR, PACK, PAIR]
-        speeds[0] = later[:, 3 * piece :].rearrange("p (s c t i) -> p s c t i", s=STEPS, t=PACK, i=PAIR)
-        speeds[1] = keep.tile(speed_shape, F32, name="speeds1")
-        for bank in banks[PACK:LEAD]:
-            current(*bank)
-        wl_codes = late.tile([P, R_BLOCKS, N], I32, name="wl_codes", offset=WF_FIRST + EDGE, align_bytes=64)
+        round_wf(1, 0)
+
+        wl_codes = turn("wl_codes", [P, R_BLOCKS, N], I32, AT_WC0)
         nc.sync.dma_start(wl_codes[:], wl_words.rearrange("b p c i -> p b (c i)").bitcast(I32))
+        wl_planes = wc_rows[:, :, PASS : PASS + N]
         load_planes(wl_planes, wl_scales)
-        observed = mid.tile([P, N_TILES, S], F32, name="observed", offset=4 * HALF + S + 4 * PASS)
+        observed = turn("observed", [P, N_TILES, S], F32, AT_WF00)
         nc.sync.dma_start(observed[:], obs.rearrange("(u p) j -> p u j", p=P))
-        round_wf(1, 0, nc.vector.tensor_copy)
-        drags[0] = turns.tile([P, S, PACK], BF16, name="drag0", offset=4 * PASS, align_bytes=64)
+
+        drags[0] = turn("drag0", [P, S, PACK], BF16, AT_TABLE[0])
         drags[1] = keep.tile([P, S, PACK], BF16, name="drag1", align_bytes=64)
-
-        def speed_and_current(b, s):
-            speed(b, s)
-            if b == 0 and s % 2 == 1 and LEAD + s // 2 < len(banks) - PACK:
-                current(*banks[LEAD + s // 2])
-            if (b, s) == (1, PACK - 1):
-                for bank in banks[-PACK:]:
-                    current(*bank)
-
+        quantise_wf(1, 0)
+        round_wf(1, 1)
         for s in range(STEPS):
-            speed_and_current(0, s)
+            speed(0, s)
             drag(0, s)
-            if s == 0:
-                quantise_wf(1, 0)
-                wf_round[1, 1] = keep.tile([P, PACK, P, PACK], BF16, name="wf_round1_1", tag="wf_round1_0", align_bytes=64)
-                nc.gpsimd.tensor_copy(wf_round[1, 1][:], wf_raw[1, 1].rearrange("p (i m t) -> p t m i", i=PACK, t=PACK))
         quantise_wf(1, 1)
         quantise_drag(0, 0, STEPS)
 
-        bounded = late.tile([P, N_TILES * S], F32, name="bounded", offset=WF_FIRST + PIECE - EDGE)
-
+        for s in range(STEPS // 2):
+            speed(1, s)
+        current(1, 1, 0)
+        current(1, 1, 1)
+        bounded = turn("bounded", [P, N_TILES * S], F32, AT_LAST_SQUARES)
         for s in range(STEPS + 2):
+            if STEPS // 2 <= s < STEPS:
+                speed(1, s)
             if s < STEPS:
-                speed_and_current(1, s)
                 drag(1, s)
+            if s < 2:
+                current(1, 1, s + 2)
+            if s < PACK:
+                square(1, 1, s)
             for lo, hi in SPANS:
                 if hi == s:
                     quantise_drag(1, lo, hi)

@@ -35,6 +35,7 @@ BANK_BYTES = 2048
 KIB = 1024
 SPANS = [(0, 2), (2, 4), (4, 6), (6, 7), (7, 8)]
 PIECE = PACK * PASS
+LEAD = 10
 EARLY = 2
 
 
@@ -60,7 +61,7 @@ def tile_list_surge_gauge_monitor_kernel(
 
         AT_TABLE = (0, 8 * KIB)
         AT_SQUARES = 16 * KIB
-        AT_WC1 = 23 * KIB
+        AT_WC1 = 22 * KIB
         AT_TAB_ROWS = 24 * KIB
         AT_WF00 = 25 * KIB
         AT_CODES01 = 37 * KIB
@@ -69,7 +70,8 @@ def tile_list_surge_gauge_monitor_kernel(
         AT_WC0 = 47 * KIB
         AT_LAST_SQUARES = 54 * KIB
         AT_LAST_SPEED = 66 * KIB
-        AT_ROUND = {(1, 0): 50 * KIB, (1, 1): 50 * KIB}
+        AT_CODES = {(0, 0): AT_WF01 + 2 * KIB, (1, 1): AT_LAST_SPEED}
+        AT_ROUND = {(0, 1): 50 * KIB, (1, 0): 50 * KIB, (1, 1): 50 * KIB}
 
         lists = keep.tile([P, S // GROUP], U16, name="lists")
         nc.sync.dma_start(lists[:], offs)
@@ -125,21 +127,21 @@ def tile_list_surge_gauge_monitor_kernel(
         load_table(0)
         load_planes(wc_rows, wc_scales)
         load_table(1)
+        load_wc(1)
         picked = turn("picked", [P, S], U8, AT_PICKED)
         nc.vector.tensor_copy(picked[:], tab_rows[:].indirect(lists[:]))
-        for first in range(0, P, QUADRANT):
+        for first in (0, 2 * QUADRANT, QUADRANT, 3 * QUADRANT):
             nc.sync.dma_start(
                 v_planes[first : first + PLANE_ROWS, :].bitcast(I32),
                 picked[first : first + QUADRANT : 4, :].bitcast(I32),
             )
-        load_wc(1)
         order_wc_planes(0)
 
         wf_raw = {
             (0, 0): turn("wf_raw00", [P, PIECE], F32, AT_WF00),
             (0, 1): turn("wf_raw01", [P, PIECE], F32, AT_WF01),
-            (1, 0): turn("wf_raw10", [P, PIECE], F32, AT_TABLE[0]),
-            (1, 1): turn("wf_raw11", [P, PIECE], F32, AT_TABLE[1]),
+            (1, 0): turn("wf_raw10", [P, PIECE], F32, AT_TABLE[1]),
+            (1, 1): turn("wf_raw11", [P, PIECE], F32, AT_TABLE[0]),
         }
 
         def load_wf(b, g):
@@ -231,8 +233,8 @@ def tile_list_surge_gauge_monitor_kernel(
                 )
 
         def quantise_wf(b, g):
-            if (b, g) == (1, 1):
-                codes = turn("wf_codes11", [P, PASS], U32, AT_LAST_SPEED)
+            if (b, g) in AT_CODES:
+                codes = turn("wf_codes%d%d" % (b, g), [P, PASS], U32, AT_CODES[b, g])
             else:
                 codes = keep.tile([P, PASS], U32, name="wf_codes%d%d" % (b, g), align_bytes=64)
             planes = keep.tile([P, PASS], U8, name="wf_planes%d%d" % (b, g), align_bytes=64)
@@ -279,15 +281,15 @@ def tile_list_surge_gauge_monitor_kernel(
                 in_=drags[b][:, gauges, :].rearrange("p j t -> p (j t)"),
             )
 
-        def innovation(lo, hi):
+        def level(lo, hi):
             gauges = slice(lo * STEP, hi * STEP)
             width = (hi - lo) * STEP
             per_bank = min(N_TILES, HALF // width)
-            gap = keep.tile([P, N_TILES, width], F32, name="gap%d" % lo)
+            banks = []
             for first in range(0, N_TILES, per_bank):
-                tiles = range(first, min(first + per_bank, N_TILES))
-                number, bank = take_bank([P, len(tiles), width])
-                for u in tiles:
+                rows = slice(first, min(first + per_bank, N_TILES))
+                number, bank = take_bank([P, rows.stop - first, width])
+                for u in range(first, rows.stop):
                     for b in range(R_BLOCKS):
                         nc.tensor.matmul_mx(
                             out=bank[:, u - first, :],
@@ -298,17 +300,25 @@ def tile_list_surge_gauge_monitor_kernel(
                             start=(b == 0),
                             stop=(b == R_BLOCKS - 1),
                         )
-                rows = slice(tiles.start, tiles.stop)
-                nc.vector.tensor_tensor(gap[:, rows, :], observed[:, rows, gauges], bank[:], ALU.subtract)
-                free_banks.append(number)
-            result = bounded[:, N_TILES * lo * STEP : N_TILES * hi * STEP].rearrange("p (u j) -> p u j", u=N_TILES)
-            nc.scalar.activation(result, gap[:], ACT.Tanh)
-            nc.sync.dma_start(out.rearrange("(u p) j -> p u j", p=P)[:, :, gauges], result)
+                banks.append((number, bank, rows, gauges))
+            return banks
 
-        for b, half in ((0, 0), (0, 1), (1, 0)):
-            for t in range(PACK):
-                current(b, half, t)
-                square(b, half, t)
+        def innovation(number, bank, rows, gauges):
+            width = gauges.stop - gauges.start
+            half, start = divmod(gauges.start, HALF)
+            gap = keep.tile([P, rows.stop - rows.start, width], F32, name="gap%d_%d" % (gauges.start, rows.start))
+            nc.vector.tensor_tensor(gap[:], observed[half][:, rows, start : start + width], bank[:], ALU.subtract)
+            free_banks.append(number)
+            place = N_TILES * gauges.start
+            result = bounded[:, place : place + N_TILES * width].rearrange("p (u j) -> p u j", u=N_TILES)
+            nc.scalar.activation(result[:, rows], gap[:], ACT.Tanh)
+            nc.sync.dma_start(out.rearrange("(u p) j -> p u j", p=P)[:, rows, gauges], result[:, rows])
+
+        leading = [(b, half, t) for b, half in ((0, 0), (0, 1), (1, 0)) for t in range(PACK)]
+        for n, bank in enumerate(leading):
+            current(*bank)
+            if n < LEAD:
+                square(*bank)
         round_wf(0, 0)
         round_wf(0, 1)
         quantise_wf(0, 0)
@@ -319,35 +329,46 @@ def tile_list_surge_gauge_monitor_kernel(
         nc.sync.dma_start(wl_codes[:], wl_words.rearrange("b p c i -> p b (c i)").bitcast(I32))
         wl_planes = wc_rows[:, :, PASS : PASS + N]
         load_planes(wl_planes, wl_scales)
-        observed = turn("observed", [P, N_TILES, S], F32, AT_WF00)
-        nc.sync.dma_start(observed[:], obs.rearrange("(u p) j -> p u j", p=P))
+        observed = []
+        for half in range(HALVES):
+            observed.append(turn("observed%d" % half, [P, N_TILES, HALF], F32, AT_WF00 + half * 4 * N_TILES * HALF))
+            nc.sync.dma_start(
+                observed[half][:], obs.rearrange("(u p) j -> p u j", p=P)[:, :, half * HALF : (half + 1) * HALF]
+            )
 
-        drags[0] = turn("drag0", [P, S, PACK], BF16, AT_TABLE[0])
+        drags[0] = turn("drag0", [P, S, PACK], BF16, AT_TABLE[1])
         drags[1] = keep.tile([P, S, PACK], BF16, name="drag1", align_bytes=64)
         quantise_wf(1, 0)
         round_wf(1, 1)
         for s in range(STEPS):
             speed(0, s)
             drag(0, s)
+        for bank in leading[LEAD:]:
+            square(*bank)
         quantise_wf(1, 1)
         quantise_drag(0, 0, STEPS)
 
         for s in range(STEPS // 2):
             speed(1, s)
-        current(1, 1, 0)
-        current(1, 1, 1)
+        for t in range(PACK - 1):
+            current(1, 1, t)
         bounded = turn("bounded", [P, N_TILES * S], F32, AT_LAST_SQUARES)
-        for s in range(STEPS + 2):
-            if STEPS // 2 <= s < STEPS:
+        waiting = []
+        for s in range(STEPS):
+            if s >= STEPS // 2:
                 speed(1, s)
-            if s < STEPS:
-                drag(1, s)
-            if s < 2:
-                current(1, 1, s + 2)
+            drag(1, s)
+            if s == 0:
+                current(1, 1, PACK - 1)
             if s < PACK:
                 square(1, 1, s)
-            for lo, hi in SPANS:
-                if hi == s:
-                    quantise_drag(1, lo, hi)
-                if hi + 1 == s:
-                    innovation(lo, hi)
+            if s > 0 and s % 2 == 0:
+                quantise_drag(1, s - 2, s)
+            if s == STEPS // 2 - 1:
+                waiting = level(*SPANS[0])
+            if s % (STEPS // 2) == STEPS // 2 - 1:
+                innovation(*waiting.pop(0))
+        quantise_drag(1, STEPS - 2, STEPS)
+        for span in SPANS[1:]:
+            for bank in level(*span):
+                innovation(*bank)

@@ -36,6 +36,7 @@ KIB = 1024
 SPANS = [(0, 2), (2, 4), (4, 6), (6, 7), (7, 8)]
 PIECE = PACK * PASS
 LEAD = 10
+EARLY_WARM_UPS, LATE_WARM_UPS = 3, 3
 EARLY = 2
 
 
@@ -70,7 +71,7 @@ def tile_list_surge_gauge_monitor_kernel(
         AT_WC0 = 47 * KIB
         AT_LAST_SQUARES = 54 * KIB
         AT_LAST_SPEED = 66 * KIB
-        AT_CODES = {(0, 0): AT_WF01 + 2 * KIB, (1, 1): AT_LAST_SPEED}
+        AT_CODES = {(1, 1): AT_LAST_SPEED}
         AT_ROUND = {(0, 1): 50 * KIB, (1, 0): 50 * KIB, (1, 1): 50 * KIB}
 
         lists = keep.tile([P, S // GROUP], U16, name="lists")
@@ -163,6 +164,18 @@ def tile_list_surge_gauge_monitor_kernel(
         load_wf(0, 0)
         load_wf(0, 1)
         gather(0, 0)
+        number, bank = take_bank([P, HALF])
+        for words in [table[0][:, :HALF]] * EARLY_WARM_UPS + [v_codes[0, 0][:]] * LATE_WARM_UPS:
+            nc.tensor.matmul_mx(
+                out=bank[:],
+                lhsT=wc_codes[0][:, 0, : 2 * P].bitcast(FP4X4),
+                lhsT_scale=wc_rows[:, 0, :P],
+                rhs=words.bitcast(FP8X4),
+                rhs_scale=wc_rows[:, 0, :HALF],
+                start=True,
+                stop=True,
+            )
+        free_banks.append(number)
         order_wc_planes(1)
         gather(1, 0)
         gather(1, 1)
@@ -182,7 +195,7 @@ def tile_list_surge_gauge_monitor_kernel(
         def current(b, half, t):
             currents[b, half, t] = take_bank([P, HALF])
             bank = currents[b, half, t][1]
-            passes = (0, 1) if len(made) <= EARLY else (1, 0)
+            passes = (0, 1) if len(currents) <= EARLY else (1, 0)
             for g in passes:
                 nc.tensor.matmul_mx(
                     out=bank[:],
@@ -320,8 +333,8 @@ def tile_list_surge_gauge_monitor_kernel(
             if n < LEAD:
                 square(*bank)
         round_wf(0, 0)
-        round_wf(0, 1)
         quantise_wf(0, 0)
+        round_wf(0, 1)
         quantise_wf(0, 1)
         round_wf(1, 0)
 

@@ -33,7 +33,7 @@ N_TILES = N // P
 BANKS = 8
 BANK_BYTES = 2048
 KIB = 1024
-SPANS = [(0, 2), (2, 4), (4, 6), (6, 7), (7, 8)]
+SPANS = [(0, 2), (2, 4), (4, 6), (6, 8)]
 PIECE = PACK * PASS
 LEAD = 10
 EARLY_WARM_UPS, LATE_WARM_UPS = 3, 3
@@ -89,22 +89,19 @@ def tile_list_surge_gauge_monitor_kernel(
         nc.scalar.activation(background[:], one[:], ACT.Sqrt)
 
         table = [turn("table%d" % g, [P, T], I32, AT_TABLE[g]) for g in range(K_PASSES)]
-        wc_hbm = wc_words.rearrange("g p c -> p g c").bitcast(I32)
         wc_raw = [turn("wc_raw0", [P, PASS], I32, AT_WC0), turn("wc_raw1", [P, PASS], I32, AT_WC1)]
         wc_codes = [keep.tile([P, K_PASSES, 2 * PASS], U8, name="wc_codes%d" % b, align_bytes=64) for b in range(R_BLOCKS)]
 
         def load_table(g):
             nc.sync.dma_start(table[g][:], tab_words[g].rearrange("p t i -> p (t i)").bitcast(I32))
 
-        def load_wc(b):
-            nc.sync.dma_start(
-                wc_raw[b][:].rearrange("p (g c) -> p g c", g=K_PASSES),
-                wc_hbm[:, :, b * PASS // 2 : (b + 1) * PASS // 2],
-            )
-            nc.scalar.copy(
-                wc_codes[b][:].bitcast(U16).rearrange("p g (t m) -> p g t m", t=PACK),
-                wc_raw[b][:].bitcast(U16).rearrange("p (g m t) -> p g t m", g=K_PASSES, t=PACK),
-            )
+        def load_wc(g):
+            nc.sync.dma_start(wc_raw[g][:], wc_words[g].bitcast(I32))
+            for b in range(R_BLOCKS):
+                nc.scalar.copy(
+                    wc_codes[b][:, g].bitcast(U16).rearrange("p (t m) -> p t m", t=PACK),
+                    wc_raw[g][:].bitcast(U16)[:, b * PASS : (b + 1) * PASS].rearrange("p (m t) -> p t m", t=PACK),
+                )
 
         def load_planes(planes, scales):
             for e in range(PLANE_ROWS):
@@ -319,12 +316,15 @@ def tile_list_surge_gauge_monitor_kernel(
         def innovation(number, bank, rows, gauges):
             width = gauges.stop - gauges.start
             half, start = divmod(gauges.start, HALF)
-            gap = keep.tile([P, rows.stop - rows.start, width], F32, name="gap%d_%d" % (gauges.start, rows.start))
-            nc.vector.tensor_tensor(gap[:], observed[half][:, rows, start : start + width], bank[:], ALU.subtract)
-            free_banks.append(number)
             place = N_TILES * gauges.start
             result = bounded[:, place : place + N_TILES * width].rearrange("p (u j) -> p u j", u=N_TILES)
-            nc.scalar.activation(result[:, rows], gap[:], ACT.Tanh)
+            for u in range(rows.start, rows.stop):
+                gap = keep.tile([P, width], F32, name="gap%d_%d" % (gauges.start, u))
+                nc.vector.tensor_tensor(
+                    gap[:], observed[half][:, u, start : start + width], bank[:, u - rows.start], ALU.subtract
+                )
+                nc.scalar.activation(result[:, u], gap[:], ACT.Tanh)
+            free_banks.append(number)
             nc.sync.dma_start(out.rearrange("(u p) j -> p u j", p=P)[:, rows, gauges], result[:, rows])
 
         leading = [(b, half, t) for b, half in ((0, 0), (0, 1), (1, 0)) for t in range(PACK)]

from contextlib import ExitStack

import concourse.mybir as mybir

K, T, S, H, N = 1024, 2048, 1024, 1024, 384
FLOPS = 2 * K * H * S * 2 + 2 * H * N * S

F32 = mybir.dt.float32
BF16 = mybir.dt.bfloat16
I32 = mybir.dt.int32
U32 = mybir.dt.uint32
U16 = mybir.dt.uint16
U8 = mybir.dt.uint8
FP8X4 = mybir.dt.float8_e4m3fn_x4
FP4X4 = mybir.dt.float4_e2m1fn_x4
ACT = mybir.ActivationFunctionType
ALU = mybir.AluOpType

P = 128
PACK = 4
PASS = P * PACK
K_PASSES = K // PASS
R_BLOCKS = H // PASS
QUADRANT = 32
PLANE_ROWS = 4
GROUP = 16
HALF = 512
HALVES = S // HALF
STEP = 128
STEPS = S // STEP
PAIR = 2
N_TILES = N // P
BANKS = 8
BANK_BYTES = 2048
KIB = 1024
SPANS = [(0, 2), (2, 4), (4, 6), (6, 8)]
PIECE = PACK * PASS
LEAD = 10
EARLY_WARM_UPS, LATE_WARM_UPS = 3, 3
EARLY = 2


def tile_list_surge_gauge_monitor_kernel(
    tc, tab_words, tab_scales, offs, wc_words, wc_scales, wf, wl_words, wl_scales, obs, out
):
    nc = tc.nc
    with ExitStack() as ctx:
        keep = ctx.enter_context(tc.tile_pool(name="keep", bufs=1))
        turns = ctx.enter_context(tc.tile_pool(name="turns", bufs=1))
        psum = ctx.enter_context(tc.psum_pool(name="psum", bufs=1))

        def turn(name, shape, dtype, offset):
            return turns.tile(shape, dtype, name=name, offset=offset, align_bytes=64)

        free_banks = list(range(BANKS))
        made = []

        def take_bank(shape):
            number = free_banks.pop(0)
            made.append(number)
            return number, psum.tile(shape, F32, name="bank%d" % len(made), offset=number * BANK_BYTES)

        AT_TABLE = (0, 8 * KIB)
        AT_SQUARES = 16 * KIB
        AT_WC1 = 22 * KIB
        AT_TAB_ROWS = 24 * KIB
        AT_WF00 = 25 * KIB
        AT_CODES01 = 37 * KIB
        AT_PICKED = AT_CODES01 + 3 * KIB // 2
        AT_WF01 = AT_CODES01 + 2 * KIB
        AT_WC0 = 47 * KIB
        AT_LAST_SQUARES = 54 * KIB
        AT_LAST_SPEED = 66 * KIB
        AT_CODES = {(1, 1): AT_LAST_SPEED}
        AT_ROUND = {(0, 1): 50 * KIB, (1, 0): 50 * KIB, (1, 1): 50 * KIB}

        lists = keep.tile([P, S // GROUP], U16, name="lists")
        nc.sync.dma_start(lists[:], offs)

        tab_rows = turn("tab_rows", [P, T], U8, AT_TAB_ROWS)
        wc_rows = keep.tile([P, K_PASSES, H], U8, name="wc_rows", align_bytes=64)
        v_planes = keep.tile([P, K_PASSES * S], U8, name="v_planes", align_bytes=64)
        one = keep.tile([P, 8], F32, name="one")
        background = keep.tile([P, 8], F32, name="background")
        nc.gpsimd.memset(tab_rows[:].bitcast(I32), 0)
        nc.vector.memset(wc_rows[:].bitcast(I32), 0)
        nc.vector.memset(one[:], 1.0)
        nc.vector.memset(v_planes[:].bitcast(I32), 0)
        nc.scalar.activation(background[:], one[:], ACT.Sqrt)

        table = [turn("table%d" % g, [P, T], I32, AT_TABLE[g]) for g in range(K_PASSES)]
        wc_raw = [turn("wc_raw0", [P, PASS], I32, AT_WC0), turn("wc_raw1", [P, PASS], I32, AT_WC1)]
        wc_codes = [keep.tile([P, K_PASSES, 2 * PASS], U8, name="wc_codes%d" % b, align_bytes=64) for b in range(R_BLOCKS)]

        def load_table(g):
            nc.sync.dma_start(table[g][:], tab_words[g].rearrange("p t i -> p (t i)").bitcast(I32))

        def load_wc(g):
            nc.sync.dma_start(wc_raw[g][:], wc_words[g].bitcast(I32))
            for b in range(R_BLOCKS):
                nc.scalar.copy(
                    wc_codes[b][:, g].bitcast(U16).rearrange("p (t m) -> p t m", t=PACK),
                    wc_raw[g][:].bitcast(U16)[:, b * PASS : (b + 1) * PASS].rearrange("p (m t) -> p t m", t=PACK),
                )

        def load_planes(planes, scales):
            for e in range(PLANE_ROWS):
                nc.sync.dma_start(
                    planes[e:P:QUADRANT].bitcast(I32),
                    scales[:, e::PLANE_ROWS, :].rearrange("g d c -> d g c").bitcast(I32),
                )

        wc_planes = [keep.tile([P, K_PASSES, PASS], U8, name="wc_planes%d" % b, align_bytes=64) for b in range(R_BLOCKS)]

        def order_wc_planes(b):
            nc.vector.tensor_copy(
                wc_planes[b][:].rearrange("p g (t m) -> p g t m", t=PACK),
                wc_rows[:, :, b * PASS : (b + 1) * PASS].rearrange("p g (m t) -> p g t m", t=PACK),
            )

        load_wc(0)
        nc.sync.dma_start(
            tab_rows[0:P:4, :].bitcast(I32), tab_scales.rearrange("g q c -> q g c").bitcast(I32)
        )
        load_table(0)
        load_planes(wc_rows, wc_scales)
        load_table(1)
        load_wc(1)
        picked = turn("picked", [P, S], U8, AT_PICKED)
        nc.vector.tensor_copy(picked[:], tab_rows[:].indirect(lists[:]))
        for first in (0, 2 * QUADRANT, QUADRANT, 3 * QUADRANT):
            nc.sync.dma_start(
                v_planes[first : first + PLANE_ROWS, :].bitcast(I32),
                picked[first : first + QUADRANT : 4, :].bitcast(I32),
            )
        order_wc_planes(0)

        wf_raw = {
            (0, 0): turn("wf_raw00", [P, PIECE], F32, AT_WF00),
            (0, 1): turn("wf_raw01", [P, PIECE], F32, AT_WF01),
            (1, 0): turn("wf_raw10", [P, PIECE], F32, AT_TABLE[1]),
            (1, 1): turn("wf_raw11", [P, PIECE], F32, AT_TABLE[0]),
        }

        def load_wf(b, g):
            nc.sync.dma_start(
                wf_raw[b, g][:].rearrange("p (i c) -> p i c", i=PACK),
                wf[g * PASS : (g + 1) * PASS, b * PASS : (b + 1) * PASS].rearrange("(p i) c -> p i c", i=PACK),
            )

        v_codes = {}

        def gather(g, half):
            if (g, half) == (0, 1):
                v_codes[g, half] = turn("v_codes01", [P, HALF], U32, AT_CODES01)
            else:
                v_codes[g, half] = keep.tile([P, HALF], U32, name="v_codes%d%d" % (g, half), align_bytes=64)
            entries = lists[:, half * HALF // GROUP : (half + 1) * HALF // GROUP]
            nc.vector.tensor_copy(v_codes[g, half][:], table[g][:].bitcast(U32).indirect(entries))

        load_wf(0, 0)
        load_wf(0, 1)
        gather(0, 0)
        number, bank = take_bank([P, HALF])
        for words in [table[0][:, :HALF]] * EARLY_WARM_UPS + [v_codes[0, 0][:]] * LATE_WARM_UPS:
            nc.tensor.matmul_mx(
                out=bank[:],
                lhsT=wc_codes[0][:, 0, : 2 * P].bitcast(FP4X4),
                lhsT_scale=wc_rows[:, 0, :P],
                rhs=words.bitcast(FP8X4),
                rhs_scale=wc_rows[:, 0, :HALF],
                start=True,
                stop=True,
            )
        free_banks.append(number)
        order_wc_planes(1)
        gather(1, 0)
        gather(1, 1)
        gather(0, 1)
        load_wf(1, 0)
        load_wf(1, 1)

        square_shape = [P, HALF // 4, PACK, 2, PAIR]
        squares = {
            (0, 0): turn("squares00", square_shape, F32, AT_SQUARES),
            (0, 1): keep.tile(square_shape, F32, name="squares01"),
            (1, 0): keep.tile(square_shape, F32, name="squares10"),
            (1, 1): turn("squares11", square_shape, F32, AT_LAST_SQUARES),
        }
        currents = {}

        def current(b, half, t):
            currents[b, half, t] = take_bank([P, HALF])
            bank = currents[b, half, t][1]
            passes = (0, 1) if len(currents) <= EARLY else (1, 0)
            for g in passes:
                nc.tensor.matmul_mx(
                    out=bank[:],
                    lhsT=wc_codes[b][:, g, 2 * P * t : 2 * P * (t + 1)].bitcast(FP4X4),
                    lhsT_scale=wc_planes[b][:, g, P * t : P * (t + 1)],
                    rhs=v_codes[g, half][:].bitcast(FP8X4),
                    rhs_scale=v_planes[:, g * S + half * HALF : g * S + (half + 1) * HALF],
                    start=(g == passes[0]),
                    stop=(g == passes[-1]),
                )

        def square(b, half, t):
            number, bank = currents[b, half, t]
            nc.scalar.activation(
                squares[b, half][:, :, t], bank[:].rearrange("p (h c i) -> p c h i", h=2, i=PAIR), ACT.Square
            )
            free_banks.append(number)

        speeds = {}

        def speed(b, s):
            half, first = divmod(s * STEP, HALF)
            side, first = divmod(first, HALF // 2)
            pairs = slice(first // PAIR, (first + STEP) // PAIR)
            shape = [P, STEP // PAIR, PACK, PAIR]
            if (b, s) == (0, STEPS - 1):
                speeds[b, s] = turn("last_speed", shape, F32, AT_LAST_SPEED)
            else:
                speeds[b, s] = keep.tile(shape, F32, name="speed%d_%d" % (b, s))
            nc.scalar.activation(speeds[b, s][:], squares[b, half][:, pairs, :, side], ACT.Sqrt, bias=background[:, :1])

        wf_codes = {}
        wf_planes = {}
        wf_round = {}

        def round_wf(b, g):
            shape = [P, PACK, P, PACK]
            if (b, g) in AT_ROUND:
                wf_round[b, g] = turn("wf_round%d%d" % (b, g), shape, BF16, AT_ROUND[b, g])
            else:
                wf_round[b, g] = keep.tile(shape, BF16, name="wf_round%d%d" % (b, g), align_bytes=64)
            if (b, g) == (1, 1):
                nc.gpsimd.tensor_copy(wf_round[b, g][:], wf_raw[b, g][:].rearrange("p (i m t) -> p t m i", i=PACK, t=PACK))
            else:
                nc.vector.tensor_copy(
                    wf_round[b, g][:].rearrange("p t m i -> p m i t"),
                    wf_raw[b, g][:].rearrange("p (i m t) -> p m i t", i=PACK, t=PACK),
                )

        def quantise_wf(b, g):
            if (b, g) in AT_CODES:
                codes = turn("wf_codes%d%d" % (b, g), [P, PASS], U32, AT_CODES[b, g])
            else:
                codes = keep.tile([P, PASS], U32, name="wf_codes%d%d" % (b, g), align_bytes=64)
            planes = keep.tile([P, PASS], U8, name="wf_planes%d%d" % (b, g), align_bytes=64)
            nc.vector.quantize_mx(
                out=codes[:].bitcast(FP8X4),
                scales=planes[:],
                in_=wf_round[b, g][:].rearrange("p t m i -> p (t m i)"),
            )
            wf_codes[b, g] = codes
            wf_planes[b, g] = planes

        drags = {}
        h_codes = [keep.tile([P, S], U32, name="h_codes%d" % b, align_bytes=64) for b in range(R_BLOCKS)]
        h_planes = [keep.tile([P, S], U8, name="h_plane%d" % b, align_bytes=64) for b in range(R_BLOCKS)]

        def drag(b, s):
            gauges = slice(s * STEP, (s + 1) * STEP)
            half, first = divmod(s * STEP, HALF)
            number, bank = take_bank([P, PACK, STEP])
            for t in range(PACK):
                for g in range(K_PASSES):
                    nc.tensor.matmul_mx(
                        out=bank[:, t, :],
                        lhsT=wf_codes[b, g][:, P * t : P * (t + 1)].bitcast(FP8X4),
                        lhsT_scale=wf_planes[b, g][:, P * t : P * (t + 1)],
                        rhs=v_codes[g, half][:, first : first + STEP].bitcast(FP8X4),
                        rhs_scale=v_planes[:, g * S + s * STEP : g * S + (s + 1) * STEP],
                        start=(g == 0),
                        stop=(g == K_PASSES - 1),
                    )
            nc.vector.tensor_tensor(
                drags[b][:, gauges, :].rearrange("p (c i) t -> p c t i", i=PAIR),
                bank[:].rearrange("p t (c i) -> p c t i", i=PAIR),
                speeds[b, s][:],
                ALU.mult,
            )
            free_banks.append(number)

        def quantise_drag(b, lo, hi):
            gauges = slice(lo * STEP, hi * STEP)
            nc.vector.quantize_mx(
                out=h_codes[b][:, gauges].bitcast(FP8X4),
                scales=h_planes[b][:, gauges],
                in_=drags[b][:, gauges, :].rearrange("p j t -> p (j t)"),
            )

        def level(lo, hi):
            gauges = slice(lo * STEP, hi * STEP)
            width = (hi - lo) * STEP
            per_bank = min(N_TILES, HALF // width)
            banks = []
            for first in range(0, N_TILES, per_bank):
                rows = slice(first, min(first + per_bank, N_TILES))
                number, bank = take_bank([P, rows.stop - first, width])
                for u in range(first, rows.stop):
                    for b in range(R_BLOCKS):
                        nc.tensor.matmul_mx(
                            out=bank[:, u - first, :],
                            lhsT=wl_codes[:, b, P * u : P * (u + 1)].bitcast(FP8X4),
                            lhsT_scale=wl_planes[:, b, P * u : P * (u + 1)],
                            rhs=h_codes[b][:, gauges].bitcast(FP8X4),
                            rhs_scale=h_planes[b][:, gauges],
                            start=(b == 0),
                            stop=(b == R_BLOCKS - 1),
                        )
                banks.append((number, bank, rows, gauges))
            return banks

        def innovation(number, bank, rows, gauges):
            width = gauges.stop - gauges.start
            half, start = divmod(gauges.start, HALF)
            place = N_TILES * gauges.start
            result = bounded[:, place : place + N_TILES * width].rearrange("p (u j) -> p u j", u=N_TILES)
            for u in range(rows.start, rows.stop):
                gap = keep.tile([P, width], F32, name="gap%d_%d" % (gauges.start, u))
                nc.vector.tensor_tensor(
                    gap[:], observed[half][:, u, start : start + width], bank[:, u - rows.start], ALU.subtract
                )
                nc.scalar.activation(result[:, u], gap[:], ACT.Tanh)
            free_banks.append(number)
            nc.sync.dma_start(out.rearrange("(u p) j -> p u j", p=P)[:, rows, gauges], result[:, rows])

        leading = [(b, half, t) for b, half in ((0, 0), (0, 1), (1, 0)) for t in range(PACK)]
        for n, bank in enumerate(leading):
            current(*bank)
            if n < LEAD:
                square(*bank)
        round_wf(0, 0)
        quantise_wf(0, 0)
        round_wf(0, 1)
        quantise_wf(0, 1)
        round_wf(1, 0)

        wl_codes = turn("wl_codes", [P, R_BLOCKS, N], I32, AT_WC0)
        nc.sync.dma_start(wl_codes[:], wl_words.rearrange("b p c i -> p b (c i)").bitcast(I32))
        wl_planes = wc_rows[:, :, PASS : PASS + N]
        load_planes(wl_planes, wl_scales)
        observed = []
        for half in range(HALVES):
            observed.append(turn("observed%d" % half, [P, N_TILES, HALF], F32, AT_WF00 + half * 4 * N_TILES * HALF))
            nc.sync.dma_start(
                observed[half][:], obs.rearrange("(u p) j -> p u j", p=P)[:, :, half * HALF : (half + 1) * HALF]
            )

        drags[0] = turn("drag0", [P, S, PACK], BF16, AT_TABLE[1])
        drags[1] = keep.tile([P, S, PACK], BF16, name="drag1", align_bytes=64)
        quantise_wf(1, 0)
        round_wf(1, 1)
        for s in range(STEPS):
            speed(0, s)
            drag(0, s)
        for bank in leading[LEAD:]:
            square(*bank)
        quantise_wf(1, 1)
        quantise_drag(0, 0, STEPS)

        for s in range(STEPS // 2):
            speed(1, s)
        for t in range(PACK - 1):
            current(1, 1, t)
        bounded = turn("bounded", [P, N_TILES * S], F32, AT_LAST_SQUARES)
        waiting = []
        for s in range(STEPS):
            if s >= STEPS // 2:
                speed(1, s)
            drag(1, s)
            if s == 0:
                current(1, 1, PACK - 1)
            if s < PACK:
                square(1, 1, s)
            if s > 0 and s % 2 == 0:
                quantise_drag(1, s - 2, s)
            if s == STEPS // 2 - 1:
                waiting = level(*SPANS[0])
            if s % (STEPS // 2) == STEPS // 2 - 1:
                innovation(*waiting.pop(0))
        quantise_drag(1, STEPS - 2, STEPS)
        for span in SPANS[1:]:
            for bank in level(*span):
                innovation(*bank)
